import numpy as np
import ml_dtypes


def mxq(x, axis, fmt="e4m3"):
    dtype, down = {"e4m3": (ml_dtypes.float8_e4m3fn, 7), "e5m2": (ml_dtypes.float8_e5m2, 14)}[fmt]
    v = np.moveaxis(np.asarray(x, np.float32).astype(ml_dtypes.bfloat16).astype(np.float64), axis, -1)
    blocks = v.reshape(v.shape[:-1] + (-1, 32))
    amax = np.abs(blocks).max(-1, keepdims=True)
    byte = np.maximum(np.where(amax > 0, np.frexp(amax)[1] - 1 + 127, 0) - down, 1)
    scale = np.exp2(byte - 127.0)
    codes = (blocks / scale).astype(np.float32).astype(dtype).astype(np.float64)
    return np.moveaxis((codes * scale).reshape(v.shape), -1, axis)


WIDE = False


def mx_kscale(k):
    if not WIDE:
        return np.ones(k)
    levels = np.array([10, -10, 5, -5, 0])
    if k % 512:
        return np.exp2(np.random.permutation(np.resize(levels, k // 32))).repeat(32)
    a = np.empty((k // 512, 16))
    for p in range(k // 512):
        a[p, :8] = np.random.permutation(np.resize(levels, 8))
        for g in range(8):
            far = levels[np.abs(levels - a[p, g]) >= 10]
            a[p, g + 8] = far[np.random.randint(len(far))]
    return np.exp2(a.ravel()).repeat(32)


BF16 = ml_dtypes.bfloat16


def bf(x):
    return np.asarray(x, np.float32).astype(BF16)


def f64(x):
    return np.asarray(x).astype(np.float64)


E2M1 = np.array([0.0, 0.5, 1.0, 1.5, 2.0, 3.0, 4.0, 6.0, -0.0, -0.5, -1.0, -1.5, -2.0, -3.0, -4.0, -6.0])


def pack_weight(w, fmt):
    k, n = w.shape
    w = f64(bf(w)).reshape(k // 32, 32, n)
    amax = np.abs(w).max(1)
    if fmt == "e4m3":
        byte = np.frexp(amax)[1] - 1 + 127 - 7
    else:
        mant, ex = np.frexp(amax / 6.0)
        byte = np.where(mant > 0.5, ex, ex - 1) + 127
    byte = np.clip(np.where(amax > 0, byte, 1), 1, 254)
    scaled = (w * np.exp2(127.0 - byte)[:, None, :]).reshape(k, n).astype(np.float32)
    by_word = np.ascontiguousarray(scaled.reshape(k // 512, 128, 4, n).transpose(0, 1, 3, 2))
    if fmt == "e4m3":
        words = by_word.astype(ml_dtypes.float8_e4m3fn).view(np.uint8)
    else:
        c = by_word.astype(ml_dtypes.float4_e2m1fn).view(np.uint8) & 0xF
        words = c[..., 0::2] | (c[..., 1::2] << 4)
    return np.ascontiguousarray(words), np.ascontiguousarray(byte.astype(np.uint8).reshape(k // 512, 16, n))


def unpack_weight(words, scales, fmt):
    g, p, n, _ = words.shape
    if fmt == "e4m3":
        vals = np.ascontiguousarray(words).view(ml_dtypes.float8_e4m3fn).astype(np.float64)
    else:
        nib = np.empty((g, p, n, 4), np.uint8)
        nib[..., 0::2] = words & 0xF
        nib[..., 1::2] = words >> 4
        vals = E2M1[nib]
    vals = vals * np.repeat(np.exp2(scales.astype(np.float64) - 127.0), 8, axis=1)[..., None]
    return vals.transpose(0, 1, 3, 2).reshape(g * 512, n)
def pack4(w):
    words, scales = pack_weight(w, "e2m1")
    return words.reshape(words.shape[0], 128, -1), scales


def unpack4(words, scales):
    return unpack_weight(words.reshape(words.shape[0], 128, -1, 2), scales, "e2m1")


M, N, R = 2048, 3072, 256

NOISE = 0.5


def draw0():
    s, t = mx_kscale(M), mx_kscale(N)
    A = np.random.standard_normal((M, N)) / np.sqrt(M)
    at_words, at_scales = pack4(A.T / t[:, None])
    return {"a": bf(A * s[:, None]),
            "omega": bf(np.random.standard_normal((M, R)) / s[:, None]),
            "sample_w": bf((1 + 0.1 * np.random.standard_normal(N)) * t),
            "noise_var": bf(NOISE * (1 + 0.1 * np.random.standard_normal(M)) * s),
            "at_words": at_words,
            "at_scales": at_scales}


def core(a, omega, sample_w, noise_var, at_words, at_scales):
    om = f64(omega)
    z = mxq(f64(a), 0, "e4m3").T @ mxq(om, 0, "e4m3")
    zw = z * f64(sample_w)[:, None]
    y = unpack4(at_words, at_scales).T @ mxq(zw, 0, "e4m3")
    return y - f64(noise_var)[:, None] * om


def e4m3fn_bytes(y):
    return np.clip(np.asarray(y, np.float64), -448.0, 448.0).astype(np.float32).astype(ml_dtypes.float8_e4m3fn).view(np.uint8)


def e4m3fn_values(b):
    return np.asarray(b, np.uint8).view(ml_dtypes.float8_e4m3fn).astype(np.float64)


def setup_inputs():
    d = draw0()
    x0 = np.asarray(d['a']).astype(np.float64)
    s = (np.max(np.abs(x0), axis=(1,), keepdims=True) / 448.0).astype(np.float32)
    out = {}
    for k, v in d.items():
        if k == 'a':
            out['a_bytes'] = e4m3fn_bytes(x0 / s.astype(np.float64))
            out['a_scale'] = s
        else:
            out[k] = v
    return out


def reference(a_bytes, a_scale, omega, sample_w, noise_var, at_words, at_scales):
    return core(e4m3fn_values(a_bytes) * a_scale.astype(np.float64), omega, sample_w, noise_var, at_words, at_scales)

@@ -1,0 +1,294 @@
+from contextlib import ExitStack
+
+import concourse.mybir as mybir
+from concourse.masks import make_identity
+
+M, N, R = 2048, 3072, 256
+FLOPS = 2 * 2 * M * N * R
+
+F32 = mybir.dt.float32
+BF16 = mybir.dt.bfloat16
+U32 = mybir.dt.uint32
+I32 = mybir.dt.int32
+U8 = mybir.dt.uint8
+FP8 = mybir.dt.float8_e4m3fn
+FP8X4 = mybir.dt.float8_e4m3fn_x4
+FP4X4 = mybir.dt.float4_e2m1fn_x4
+MULT = mybir.AluOpType.mult
+ADD = mybir.AluOpType.add
+COPY = mybir.ActivationFunctionType.Copy
+
+P = 128
+PACK = 4
+KG = M // 512
+NG = N // 512
+S = 512
+MT = M // P
+PAIRS = MT // 2
+NACC = 6
+LATE = (6, 7)
+LAST = NG - 1
+
+UNITS = NG * KG
+BLOCKS = S // 8
+V_BLOCKS = {0: 24, 23: 32, 16: 48, 21: 16, 11: 24, 5: 32, 17: 32, 19: 8, 20: 48, 7: 48}
+S_PLANES = {0: (3,), 20: (3,), 2: (2, 3), 12: (3,), 18: (2, 3), 22: (1, 2, 3), 9: (1, 2, 3), 23: (3,), 13: (3,), 21: (3,), 7: (3,)}
+
+
+def tile_weighted_range_power_step_s13_kernel(
+    tc, a_bytes, a_scale, omega, sample_w, noise_var, at_words, at_scales, out
+):
+    nc = tc.nc
+    with ExitStack() as ctx:
+        keep = ctx.enter_context(tc.tile_pool(name="keep", bufs=1))
+        work = ctx.enter_context(tc.tile_pool(name="work", bufs=3))
+        psum = ctx.enter_context(tc.psum_pool(name="psum", bufs=1))
+        ctx.enter_context(tc.manual_schedule())
+
+        a_raw = {
+            (g, k): keep.tile([P, PACK, S], U8, name="a_raw%d_%d" % (g, k), align_bytes=64)
+            for g in range(NG)
+            for k in range(KG)
+        }
+        om_raw = [keep.tile([P, PACK, R], BF16, name="om_raw%d" % k, align_bytes=64) for k in range(KG)]
+        om_codes = [keep.tile([P, R], U32, name="om_codes%d" % k, align_bytes=64) for k in range(KG)]
+        om_scales = [keep.tile([P, R], U8, name="om_scales%d" % k, align_bytes=64) for k in range(KG)]
+        v_codes = [keep.tile([P, R], U32, name="v_codes%d" % g, align_bytes=64) for g in range(NG)]
+        v_scales = [keep.tile([P, R], U8, name="v_scales%d" % g, align_bytes=64) for g in range(NG)]
+        b_words = [keep.tile([P, 2 * M], U8, name="b_words%d" % g, align_bytes=64) for g in range(NG)]
+        b_scales = keep.tile([P, NG, M], U8, name="b_scales", align_bytes=64)
+        om_rows = keep.tile([P, MT, R], BF16, name="om_rows", align_bytes=64)
+        asc = keep.tile([P, KG, PACK], F32, name="asc")
+        w_sb = keep.tile([P, NG, PACK], BF16, name="w_sb")
+        nz = keep.tile([P, P], BF16, name="nz")
+        ident = keep.tile([P, P], BF16, name="ident")
+        neg_noise = keep.tile([P, MT], F32, name="neg_noise")
+
+        a_view = a_bytes.rearrange("(k p j) n -> k p j n", p=P, j=PACK)
+        om_view = omega.rearrange("(k p j) r -> k p j r", p=P, j=PACK)
+        scale_view = at_scales.bitcast(I32).rearrange("g q n -> q g n")
+
+        def load_a(g, k):
+            nc.sync.dma_start(out=a_raw[g, k][:], in_=a_view[k][:, :, S * g : S * (g + 1)])
+
+        def load_om(k):
+            nc.sync.dma_start(out=om_raw[k][:], in_=om_view[k])
+
+        def load_bs(q):
+            nc.sync.dma_start(out=b_scales[32 * q : 32 * q + 4].bitcast(I32), in_=scale_view[4 * q : 4 * q + 4])
+
+        def load_b(g):
+            nc.sync.dma_start(out=b_words[g][:], in_=at_words[g])
+
+        nc.scalar.dma_start(out=asc[:], in_=a_scale.rearrange("(k p j) o -> p k (j o)", p=P, j=PACK))
+        nc.vector.memset(b_scales[:].rearrange("p g n -> p (g n)").bitcast(I32), 0)
+        nc.gpsimd.memset(nz[:], 0.0)
+        make_identity(nc, ident[:])
+
+        load_a(0, 0)
+        load_om(0)
+        load_a(0, 1)
+        load_om(1)
+        load_a(0, 2)
+        load_a(0, 3)
+        load_om(2)
+        load_om(3)
+        load_a(1, 0)
+        load_a(1, 1)
+        nc.sync.dma_start(out=nz[0:MT, :], in_=noise_var.rearrange("(m p) -> m p", p=P))
+        nc.sync.dma_start(out=w_sb[:], in_=sample_w.rearrange("(g p j) -> p g j", p=P, j=PACK))
+        load_a(1, 2)
+        load_a(1, 3)
+        load_bs(0)
+        load_a(2, 0)
+        load_bs(1)
+        load_a(2, 1)
+        load_bs(2)
+        load_a(2, 2)
+        load_bs(3)
+        load_a(2, 3)
+        load_b(0)
+        load_a(3, 0)
+        load_a(3, 1)
+        load_b(1)
+        load_a(3, 2)
+        load_a(3, 3)
+        load_b(2)
+        load_a(4, 0)
+        load_a(4, 1)
+        load_a(4, 2)
+        load_a(4, 3)
+        load_b(3)
+        load_b(4)
+        nc.sync.dma_start(out=om_rows[:], in_=omega.rearrange("(m p) r -> p m r", p=P))
+        load_a(5, 0)
+        load_a(5, 1)
+        load_a(5, 2)
+        load_a(5, 3)
+        load_b(5)
+
+        planes, grouped, a_codes, a_scales = {}, {}, {}, {}
+        z, acc, v_grouped = {}, {}, {}
+
+        def widen(u):
+            g, k = divmod(u, KG)
+            planes[u] = work.tile([P, PACK, S], BF16, name="wide", bufs=5, align_bytes=64)
+            for j in range(PACK):
+                in_ = a_raw[g, k][:, j, :].bitcast(FP8)
+                if j in S_PLANES.get(u, ()):
+                    nc.scalar.activation(planes[u][:, j, :], in_, COPY, scale=asc[:, k, j : j + 1])
+                else:
+                    nc.vector.tensor_scalar(planes[u][:, j, :], in_, asc[:, k, j : j + 1], None, MULT)
+
+        def interleave(u):
+            wide = planes.pop(u)
+            grouped[u] = work.tile([P, S * PACK], BF16, name="dst_tile", bufs=4, align_bytes=64)
+            cut = BLOCKS - V_BLOCKS.get(u, 0)
+            if cut > 0:
+                src = wide[:].rearrange("p j (m i t) -> p m j i t", i=2, t=PACK)
+                dst = grouped[u][:].rearrange("p (t m i j) -> p m j i t", t=PACK, i=2, j=PACK)
+                nc.scalar.copy(dst[:, :cut], src[:, :cut])
+            if cut < BLOCKS:
+                src = wide[:].rearrange("p j (m i t) -> p m t i j", i=2, t=PACK)
+                dst = grouped[u][:].rearrange("p (t m i j) -> p m t i j", t=PACK, i=2, j=PACK)
+                nc.vector.tensor_copy(dst[:, cut:], src[:, cut:])
+
+        def quantize_a(u):
+            a_codes[u] = work.tile([P, S], U32, name="codes", bufs=6, align_bytes=64)
+            a_scales[u] = work.tile([P, S], U8, name="scales", bufs=6, align_bytes=64)
+            nc.vector.quantize_mx(a_codes[u][:].bitcast(FP8X4), a_scales[u][:], grouped.pop(u)[:])
+
+        def omega_group(k):
+            om_grouped = work.tile([P, R * PACK], BF16, name="om_grouped", bufs=2, align_bytes=64)
+            nc.vector.tensor_copy(
+                om_grouped[:].rearrange("p (c j) -> p c j", j=PACK), om_raw[k][:].rearrange("p j c -> p c j")
+            )
+            return om_grouped
+
+        def omega_quantize(k, om_grouped):
+            nc.vector.quantize_mx(om_codes[k][:].bitcast(FP8X4), om_scales[k][:], om_grouped[:])
+
+        def project(u):
+            g, k = divmod(u, KG)
+            codes, scales = a_codes.pop(u), a_scales.pop(u)
+            for h in range(2):
+                if k == 0:
+                    z[g, h] = psum.tile([P, PACK, P], F32, name="z%d_%d" % (g, h), tag="z%d" % h)
+                for t in range(PACK):
+                    nc.tensor.matmul_mx(
+                        out=z[g, h][:, t, :],
+                        lhsT=codes[:, P * t : P * (t + 1)].bitcast(FP8X4),
+                        lhsT_scale=scales[:, P * t : P * (t + 1)],
+                        rhs=om_codes[k][:, P * h : P * (h + 1)].bitcast(FP8X4),
+                        rhs_scale=om_scales[k][:, P * h : P * (h + 1)],
+                        start=(k == 0 and t == 0),
+                        stop=(k == KG - 1 and t == PACK - 1),
+                    )
+
+        HALF = P * PACK
+
+        def weigh(g):
+            v_grouped[g] = work.tile([P, R * PACK], BF16, name="v_grouped", bufs=2, align_bytes=64)
+            for h in range(2):
+                nc.vector.tensor_tensor(
+                    v_grouped[g][:, HALF * h : HALF * (h + 1)].rearrange("p (n j) -> p n j", j=PACK),
+                    z[g, h][:].rearrange("p j n -> p n j"),
+                    w_sb[:, g : g + 1, :].to_broadcast([P, P, PACK]),
+                    MULT,
+                )
+
+        def quantize_v(g, pieces):
+            width = R // pieces
+            for i in range(pieces):
+                cols = slice(width * i, width * (i + 1))
+                nc.vector.quantize_mx(
+                    v_codes[g][:, cols].bitcast(FP8X4),
+                    v_scales[g][:, cols],
+                    v_grouped[g][:, PACK * width * i : PACK * width * (i + 1)],
+                )
+
+        def back(pair, g, i, h, first, last):
+            m = 2 * pair + i
+            nc.tensor.matmul_mx(
+                out=acc[pair][:, i, P * h : P * (h + 1)],
+                lhsT=b_words[g][:, 2 * P * m : 2 * P * (m + 1)].bitcast(FP4X4),
+                lhsT_scale=b_scales[:, g, P * m : P * (m + 1)],
+                rhs=v_codes[g][:, P * h : P * (h + 1)].bitcast(FP8X4),
+                rhs_scale=v_scales[g][:, P * h : P * (h + 1)],
+                start=first,
+                stop=last,
+            )
+
+        def back_pair(pair, g, tag=None):
+            if tag is not None:
+                acc[pair] = psum.tile([P, 2, R], F32, name="acc%d_%d" % (pair, g), tag=tag)
+            closes = g == LAST
+            for h in range(2):
+                for i in range(2):
+                    back(pair, g, i, h, tag is not None and h == 0 and i == 0, closes and h == 1 and i == 1)
+
+        out_view = out.rearrange("(b i p) r -> b p i r", i=2, p=P)
+        y = {}
+
+        def subtract(m, result):
+            nc.vector.scalar_tensor_tensor(
+                result, om_rows[:, m, :], neg_noise[:, m : m + 1], acc[m // 2][:, m % 2, :], MULT, ADD
+            )
+
+        def finish(pair):
+            y[pair] = work.tile([P, 2, R], F32, name="y", bufs=8)
+            for i in range(2):
+                m = 2 * pair + i
+                subtract(m, y[pair][:, i, :])
+            nc.sync.dma_start(out=out_view[pair], in_=y[pair][:])
+
+        AHEAD = 2
+        Q_FIRST = True
+        to_back = []
+        for u in range(AHEAD):
+            widen(u)
+        for s in range(UNITS + 2):
+            g_done, phase = divmod(s - 2, KG)
+            if s < UNITS:
+                interleave(s)
+            if s + AHEAD < UNITS and not Q_FIRST:
+                widen(s + AHEAD)
+            om_grouped = omega_group(s - 1) if 1 <= s <= KG else None
+            ready = [g_done - 1] if phase == 0 and g_done > 0 else []
+            for g in ready:
+                weigh(g)
+            if s >= 2:
+                quantize_a(s - 2)
+            if s + AHEAD < UNITS and Q_FIRST:
+                widen(s + AHEAD)
+            if om_grouped is not None:
+                omega_quantize(s - 1, om_grouped)
+            for g in ready:
+                quantize_v(g, 1)
+            if s == 3:
+                noise_t = psum.tile([P, P], BF16, name="noise_t", tag="acc5")
+                nc.tensor.transpose(noise_t[:], nz[:], ident[:])
+                nc.vector.tensor_scalar(neg_noise[:], noise_t[:, 0:MT], -1.0, None, MULT)
+            if s >= 2:
+                project(s - 2)
+            for g in ready:
+                to_back += [(pair, g) for pair in range(NACC)]
+            n_back = 3 if 10 <= s < 25 else 0
+            for pair, g in to_back[:n_back]:
+                back_pair(pair, g, "acc%d" % pair if g == 0 else None)
+            to_back = to_back[n_back:]
+
+        weigh(LAST)
+        quantize_v(LAST, 2)
+        for pair, g in to_back:
+            back_pair(pair, g)
+        late = [(pair, g) for pair in LATE for g in range(NG)]
+        for pair, g in late[:3]:
+            back_pair(pair, g, "z%d" % (pair - NACC) if g == 0 else None)
+        for pair in range(NACC):
+            back_pair(pair, LAST)
+            finish(pair)
+        for pair, g in late[3:]:
+            back_pair(pair, g, "z%d" % (pair - NACC) if g == 0 else None)
+            if g == LAST:
+                finish(pair)

@@ -30,9 +30,6 @@ LATE = (6, 7)
 LAST = NG - 1
 
 UNITS = NG * KG
-BLOCKS = S // 8
-V_BLOCKS = {0: 24, 23: 32, 16: 48, 21: 16, 11: 24, 5: 32, 17: 32, 19: 8, 20: 48, 7: 48}
-S_PLANES = {0: (3,), 20: (3,), 2: (2, 3), 12: (3,), 18: (2, 3), 22: (1, 2, 3), 9: (1, 2, 3), 23: (3,), 13: (3,), 21: (3,), 7: (3,)}
 
 
 def tile_weighted_range_power_step_s13_kernel(
@@ -135,7 +132,7 @@ def tile_weighted_range_power_step_s13_kernel(
             planes[u] = work.tile([P, PACK, S], BF16, name="wide", bufs=5, align_bytes=64)
             for j in range(PACK):
                 in_ = a_raw[g, k][:, j, :].bitcast(FP8)
-                if j in S_PLANES.get(u, ()):
+                if u == 0 and j == PACK - 1:
                     nc.scalar.activation(planes[u][:, j, :], in_, COPY, scale=asc[:, k, j : j + 1])
                 else:
                     nc.vector.tensor_scalar(planes[u][:, j, :], in_, asc[:, k, j : j + 1], None, MULT)
@@ -143,15 +140,12 @@ def tile_weighted_range_power_step_s13_kernel(
         def interleave(u):
             wide = planes.pop(u)
             grouped[u] = work.tile([P, S * PACK], BF16, name="dst_tile", bufs=4, align_bytes=64)
-            cut = BLOCKS - V_BLOCKS.get(u, 0)
-            if cut > 0:
-                src = wide[:].rearrange("p j (m i t) -> p m j i t", i=2, t=PACK)
-                dst = grouped[u][:].rearrange("p (t m i j) -> p m j i t", t=PACK, i=2, j=PACK)
-                nc.scalar.copy(dst[:, :cut], src[:, :cut])
-            if cut < BLOCKS:
-                src = wide[:].rearrange("p j (m i t) -> p m t i j", i=2, t=PACK)
-                dst = grouped[u][:].rearrange("p (t m i j) -> p m t i j", t=PACK, i=2, j=PACK)
-                nc.vector.tensor_copy(dst[:, cut:], src[:, cut:])
+            src = wide[:].rearrange("p j (m i t) -> p t m j i", i=2, t=PACK)
+            dst = grouped[u][:].rearrange("p (t m i j) -> p t m j i", t=PACK, i=2, j=PACK)
+            if u < UNITS - 1:
+                nc.scalar.copy(dst, src)
+            else:
+                nc.vector.tensor_copy(dst, src)
 
         def quantize_a(u):
             a_codes[u] = work.tile([P, S], U32, name="codes", bufs=6, align_bytes=64)
@@ -161,7 +155,8 @@ def tile_weighted_range_power_step_s13_kernel(
         def omega_group(k):
             om_grouped = work.tile([P, R * PACK], BF16, name="om_grouped", bufs=2, align_bytes=64)
             nc.vector.tensor_copy(
-                om_grouped[:].rearrange("p (c j) -> p c j", j=PACK), om_raw[k][:].rearrange("p j c -> p c j")
+                om_grouped[:].rearrange("p (c i j) -> p c j i", i=2, j=PACK),
+                om_raw[k][:].rearrange("p j (c i) -> p c j i", i=2),
             )
             return om_grouped
 
@@ -191,9 +186,9 @@ def tile_weighted_range_power_step_s13_kernel(
             v_grouped[g] = work.tile([P, R * PACK], BF16, name="v_grouped", bufs=2, align_bytes=64)
             for h in range(2):
                 nc.vector.tensor_tensor(
-                    v_grouped[g][:, HALF * h : HALF * (h + 1)].rearrange("p (n j) -> p n j", j=PACK),
-                    z[g, h][:].rearrange("p j n -> p n j"),
-                    w_sb[:, g : g + 1, :].to_broadcast([P, P, PACK]),
+                    v_grouped[g][:, HALF * h : HALF * (h + 1)].rearrange("p (c i j) -> p c j i", i=2, j=PACK),
+                    z[g, h][:].rearrange("p j (c i) -> p c j i", i=2),
+                    w_sb[:, g : g + 1, :].unsqueeze(3).to_broadcast([P, P // 2, PACK, 2]),
                     MULT,
                 )
 

@@ -30,6 +30,9 @@ LATE = (6, 7)
 LAST = NG - 1
 
 UNITS = NG * KG
+BLOCKS = S // 8
+SPANS = (((0,), (1, 2), (3, 4), (5,)), ((0,), (1,), (2, 3), (4, 5)))
+SPAN_OF = {(g, k): span for k in range(KG) for span in SPANS[k % 2] for g in span}
 
 
 def tile_weighted_range_power_step_s13_kernel(
@@ -43,9 +46,9 @@ def tile_weighted_range_power_step_s13_kernel(
         ctx.enter_context(tc.manual_schedule())
 
         a_raw = {
-            (g, k): keep.tile([P, PACK, S], U8, name="a_raw%d_%d" % (g, k), align_bytes=64)
-            for g in range(NG)
+            (span[0], k): keep.tile([P, PACK, S * len(span)], U8, name="a_raw%d_%d" % (span[0], k), align_bytes=64)
             for k in range(KG)
+            for span in SPANS[k % 2]
         }
         om_raw = [keep.tile([P, PACK, R], BF16, name="om_raw%d" % k, align_bytes=64) for k in range(KG)]
         om_codes = [keep.tile([P, R], U32, name="om_codes%d" % k, align_bytes=64) for k in range(KG)]
@@ -65,14 +68,16 @@ def tile_weighted_range_power_step_s13_kernel(
         om_view = omega.rearrange("(k p j) r -> k p j r", p=P, j=PACK)
         scale_view = at_scales.bitcast(I32).rearrange("g q n -> q g n")
 
-        def load_a(g, k):
-            nc.sync.dma_start(out=a_raw[g, k][:], in_=a_view[k][:, :, S * g : S * (g + 1)])
+        def load_a(g, k, rows=slice(0, PACK)):
+            nc.sync.dma_start(
+                out=a_raw[g, k][:, rows, :], in_=a_view[k][:, rows, S * g : S * (g + len(SPAN_OF[g, k]))]
+            )
 
         def load_om(k):
             nc.sync.dma_start(out=om_raw[k][:], in_=om_view[k])
 
         def load_bs(q):
-            nc.sync.dma_start(out=b_scales[32 * q : 32 * q + 4].bitcast(I32), in_=scale_view[4 * q : 4 * q + 4])
+            nc.sync.dma_start(out=b_scales[q:P:32].bitcast(I32), in_=scale_view[q:16:4])
 
         def load_b(g):
             nc.sync.dma_start(out=b_words[g][:], in_=at_words[g])
@@ -82,70 +87,63 @@ def tile_weighted_range_power_step_s13_kernel(
         nc.gpsimd.memset(nz[:], 0.0)
         make_identity(nc, ident[:])
 
-        load_a(0, 0)
-        load_om(0)
+        load_a(0, 0, slice(0, 2))
+        load_a(0, 0, slice(2, 4))
         load_a(0, 1)
-        load_om(1)
         load_a(0, 2)
+        load_om(0)
         load_a(0, 3)
-        load_om(2)
-        load_om(3)
+        load_om(1)
         load_a(1, 0)
+        load_om(2)
         load_a(1, 1)
-        nc.sync.dma_start(out=nz[0:MT, :], in_=noise_var.rearrange("(m p) -> m p", p=P))
-        nc.sync.dma_start(out=w_sb[:], in_=sample_w.rearrange("(g p j) -> p g j", p=P, j=PACK))
+        load_om(3)
         load_a(1, 2)
         load_a(1, 3)
-        load_bs(0)
-        load_a(2, 0)
-        load_bs(1)
+        nc.sync.dma_start(out=w_sb[:], in_=sample_w.rearrange("(g p j) -> p g j", p=P, j=PACK))
+        nc.sync.dma_start(out=nz[0:MT, :], in_=noise_var.rearrange("(m p) -> m p", p=P))
         load_a(2, 1)
-        load_bs(2)
-        load_a(2, 2)
-        load_bs(3)
         load_a(2, 3)
+        for q in range(4):
+            load_bs(q)
         load_b(0)
         load_a(3, 0)
-        load_a(3, 1)
-        load_b(1)
         load_a(3, 2)
-        load_a(3, 3)
-        load_b(2)
-        load_a(4, 0)
+        load_b(1)
         load_a(4, 1)
-        load_a(4, 2)
+        load_b(2)
         load_a(4, 3)
+        load_a(5, 0)
+        load_a(5, 2)
         load_b(3)
         load_b(4)
-        nc.sync.dma_start(out=om_rows[:], in_=omega.rearrange("(m p) r -> p m r", p=P))
-        load_a(5, 0)
-        load_a(5, 1)
-        load_a(5, 2)
-        load_a(5, 3)
         load_b(5)
+        nc.sync.dma_start(out=om_rows[:], in_=omega.rearrange("(m p) r -> p m r", p=P))
 
         planes, grouped, a_codes, a_scales = {}, {}, {}, {}
         z, acc, v_grouped = {}, {}, {}
 
-        def widen(u):
-            g, k = divmod(u, KG)
-            planes[u] = work.tile([P, PACK, S], BF16, name="wide", bufs=5, align_bytes=64)
-            for j in range(PACK):
-                in_ = a_raw[g, k][:, j, :].bitcast(FP8)
-                if u == 0 and j == PACK - 1:
-                    nc.scalar.activation(planes[u][:, j, :], in_, COPY, scale=asc[:, k, j : j + 1])
-                else:
-                    nc.vector.tensor_scalar(planes[u][:, j, :], in_, asc[:, k, j : j + 1], None, MULT)
-
-        def interleave(u):
-            wide = planes.pop(u)
-            grouped[u] = work.tile([P, S * PACK], BF16, name="dst_tile", bufs=4, align_bytes=64)
-            src = wide[:].rearrange("p j (m i t) -> p t m j i", i=2, t=PACK)
-            dst = grouped[u][:].rearrange("p (t m i j) -> p t m j i", t=PACK, i=2, j=PACK)
-            if u < UNITS - 1:
-                nc.scalar.copy(dst, src)
+        def widen(g, k, j):
+            if j == 0:
+                width = len(SPAN_OF[g, k])
+                planes[g, k] = work.tile([P, PACK, S * width], BF16, name="wide%d" % width, bufs=3 + width, align_bytes=64)
+            in_ = a_raw[g, k][:, j, :].bitcast(FP8)
+            if (g, k, j) == (0, 0, PACK - 1):
+                nc.scalar.activation(planes[g, k][:, j, :], in_, COPY, scale=asc[:, k, j : j + 1])
             else:
-                nc.vector.tensor_copy(dst, src)
+                nc.vector.tensor_scalar(planes[g, k][:, j, :], in_, asc[:, k, j : j + 1], None, MULT)
+
+        def interleave(u, vector_blocks):
+            g, k = divmod(u, KG)
+            first = SPAN_OF[g, k][0]
+            wide = planes[first, k][:, :, S * (g - first) : S * (g - first + 1)]
+            grouped[u] = work.tile([P, S * PACK], BF16, name="dst_tile", bufs=4, align_bytes=64)
+            src = wide.rearrange("p j (m i t) -> p m t j i", i=2, t=PACK)
+            dst = grouped[u][:].rearrange("p (t m i j) -> p m t j i", t=PACK, i=2, j=PACK)
+            cut = BLOCKS - vector_blocks
+            if cut > 0:
+                nc.scalar.copy(dst[:, :cut], src[:, :cut])
+            return (dst[:, cut:], src[:, cut:]) if cut < BLOCKS else None
 
         def quantize_a(u):
             a_codes[u] = work.tile([P, S], U32, name="codes", bufs=6, align_bytes=64)
@@ -238,52 +236,63 @@ def tile_weighted_range_power_step_s13_kernel(
             nc.sync.dma_start(out=out_view[pair], in_=y[pair][:])
 
         AHEAD = 2
-        Q_FIRST = True
+        SHARED_UNITS = 6
+        SHARED_BLOCKS = 16
+        FIRST_BACK = 10
+        BACK_PER_STEP = 2
+        LATE_EARLY = 3
+        to_widen = [(g, k, j) for g in range(NG) for k in range(KG) if SPAN_OF[g, k][0] == g for j in range(PACK)]
+
+        def widen_for(u):
+            while to_widen:
+                g, k, j = to_widen[0]
+                opens = g * KG + k
+                if opens > u + 1 or (opens == u + 1 and (len(SPAN_OF[g, k]) == 1 or j >= PACK // 2)):
+                    break
+                widen(*to_widen.pop(0))
+
         to_back = []
-        for u in range(AHEAD):
-            widen(u)
+        om_grouped = {}
+        widen_for(AHEAD - 1)
         for s in range(UNITS + 2):
-            g_done, phase = divmod(s - 2, KG)
-            if s < UNITS:
-                interleave(s)
-            if s + AHEAD < UNITS and not Q_FIRST:
-                widen(s + AHEAD)
-            om_grouped = omega_group(s - 1) if 1 <= s <= KG else None
-            ready = [g_done - 1] if phase == 0 and g_done > 0 else []
-            for g in ready:
-                weigh(g)
+            left = interleave(s, SHARED_BLOCKS if s >= UNITS - SHARED_UNITS else 0) if s < UNITS else None
+            ready = [s // KG - 1] if s % KG == 2 and s > KG else []
+            if 1 <= s <= KG:
+                om_grouped[s - 1] = omega_group(s - 1)
             if s >= 2:
                 quantize_a(s - 2)
-            if s + AHEAD < UNITS and Q_FIRST:
-                widen(s + AHEAD)
-            if om_grouped is not None:
-                omega_quantize(s - 1, om_grouped)
+            for g in ready:
+                weigh(g)
+            widen_for(s + AHEAD)
+            if left is not None:
+                nc.vector.tensor_copy(*left)
+            if 1 <= s <= KG:
+                omega_quantize(s - 1, om_grouped[s - 1])
             for g in ready:
                 quantize_v(g, 1)
-            if s == 3:
+                to_back += [(pair, g) for pair in range(NACC)]
+            if s == 8:
                 noise_t = psum.tile([P, P], BF16, name="noise_t", tag="acc5")
                 nc.tensor.transpose(noise_t[:], nz[:], ident[:])
-                nc.vector.tensor_scalar(neg_noise[:], noise_t[:, 0:MT], -1.0, None, MULT)
+                nc.scalar.activation(neg_noise[:], noise_t[:, 0:MT], COPY, scale=-1.0)
             if s >= 2:
                 project(s - 2)
-            for g in ready:
-                to_back += [(pair, g) for pair in range(NACC)]
-            n_back = 3 if 10 <= s < 25 else 0
+            n_back = BACK_PER_STEP if FIRST_BACK <= s < UNITS else 0
             for pair, g in to_back[:n_back]:
                 back_pair(pair, g, "acc%d" % pair if g == 0 else None)
             to_back = to_back[n_back:]
 
-        weigh(LAST)
-        quantize_v(LAST, 2)
         for pair, g in to_back:
             back_pair(pair, g)
+        weigh(LAST)
+        quantize_v(LAST, 2)
         late = [(pair, g) for pair in LATE for g in range(NG)]
-        for pair, g in late[:3]:
+        for pair, g in late[:LATE_EARLY]:
             back_pair(pair, g, "z%d" % (pair - NACC) if g == 0 else None)
         for pair in range(NACC):
             back_pair(pair, LAST)
             finish(pair)
-        for pair, g in late[3:]:
+        for pair, g in late[LATE_EARLY:]:
             back_pair(pair, g, "z%d" % (pair - NACC) if g == 0 else None)
             if g == LAST:
                 finish(pair)

@@ -30,6 +30,8 @@ LATE = (6, 7)
 LAST = NG - 1
 
 UNITS = NG * KG
+TENSOR_UNITS = range(0, 13)
+SCALAR_WIDENS = (0, 2, 3, 4, 6, 9, 11)
 BLOCKS = S // 8
 SPANS = (((0,), (1, 2), (3, 4), (5,)), ((0,), (1,), (2, 3), (4, 5)))
 SPAN_OF = {(g, k): span for k in range(KG) for span in SPANS[k % 2] for g in span}
@@ -121,28 +123,46 @@ def tile_weighted_range_power_step_s13_kernel(
         nc.sync.dma_start(out=om_rows[:], in_=omega.rearrange("(m p) r -> p m r", p=P))
 
         planes, grouped, a_codes, a_scales = {}, {}, {}, {}
-        z, acc, v_grouped = {}, {}, {}
+        z, acc, v_grouped, side_by_side = {}, {}, {}, {}
 
         def widen(g, k, j):
             if j == 0:
                 width = len(SPAN_OF[g, k])
                 planes[g, k] = work.tile([P, PACK, S * width], BF16, name="wide%d" % width, bufs=3 + width, align_bytes=64)
             in_ = a_raw[g, k][:, j, :].bitcast(FP8)
-            if (g, k, j) == (0, 0, PACK - 1):
+            if j == PACK - 1 and g * KG + k in SCALAR_WIDENS:
                 nc.scalar.activation(planes[g, k][:, j, :], in_, COPY, scale=asc[:, k, j : j + 1])
             else:
                 nc.vector.tensor_scalar(planes[g, k][:, j, :], in_, asc[:, k, j : j + 1], None, MULT)
 
-        def interleave(u, vector_blocks):
+        def unit_planes(u):
             g, k = divmod(u, KG)
             first = SPAN_OF[g, k][0]
-            wide = planes[first, k][:, :, S * (g - first) : S * (g - first + 1)]
+            return planes[first, k][:, :, S * (g - first) : S * (g - first + 1)]
+
+        def interleave_on_tensor(u):
+            side_by_side[u] = psum.tile([P, S // 2, PACK], BF16, name="side%d" % u, tag="acc%d" % (u % NACC))
+            for q in range(2):
+                nc.tensor.matmul(
+                    side_by_side[u][:, P * q : P * (q + 1), :].rearrange("p n j -> p j n"),
+                    lhsT=ident[:],
+                    rhs=unit_planes(u)[:, :, S // 2 + P * q : S // 2 + P * (q + 1)],
+                    start=True,
+                    stop=True,
+                )
+
+        def interleave(u, vector_blocks):
             grouped[u] = work.tile([P, S * PACK], BF16, name="dst_tile", bufs=4, align_bytes=64)
-            src = wide.rearrange("p j (m i t) -> p m t j i", i=2, t=PACK)
+            src = unit_planes(u).rearrange("p j (m i t) -> p m t j i", i=2, t=PACK)
             dst = grouped[u][:].rearrange("p (t m i j) -> p m t j i", t=PACK, i=2, j=PACK)
-            cut = BLOCKS - vector_blocks
-            if cut > 0:
-                nc.scalar.copy(dst[:, :cut], src[:, :cut])
+            cut = BLOCKS // 2 if u in side_by_side else BLOCKS - vector_blocks
+            nc.scalar.copy(dst[:, :cut], src[:, :cut])
+            if u in side_by_side:
+                nc.scalar.copy(
+                    grouped[u][:].rearrange("p (t m j) -> p t m j", t=PACK, j=PACK)[:, :, P // 2 :, :],
+                    side_by_side[u][:].rearrange("p (m t) j -> p t m j", t=PACK),
+                )
+                return None
             return (dst[:, cut:], src[:, cut:]) if cut < BLOCKS else None
 
         def quantize_a(u):
@@ -238,8 +258,8 @@ def tile_weighted_range_power_step_s13_kernel(
         AHEAD = 2
         SHARED_UNITS = 6
         SHARED_BLOCKS = 16
-        FIRST_BACK = 10
-        BACK_PER_STEP = 2
+        FIRST_BACK = 13
+        BACK_PER_STEP = 3
         LATE_EARLY = 3
         to_widen = [(g, k, j) for g in range(NG) for k in range(KG) if SPAN_OF[g, k][0] == g for j in range(PACK)]
 
@@ -254,6 +274,7 @@ def tile_weighted_range_power_step_s13_kernel(
         to_back = []
         om_grouped = {}
         widen_for(AHEAD - 1)
+        interleave_on_tensor(0)
         for s in range(UNITS + 2):
             left = interleave(s, SHARED_BLOCKS if s >= UNITS - SHARED_UNITS else 0) if s < UNITS else None
             ready = [s // KG - 1] if s % KG == 2 and s > KG else []
@@ -271,13 +292,15 @@ def tile_weighted_range_power_step_s13_kernel(
             for g in ready:
                 quantize_v(g, 1)
                 to_back += [(pair, g) for pair in range(NACC)]
-            if s == 8:
+            if s + 1 in TENSOR_UNITS:
+                interleave_on_tensor(s + 1)
+            if s == FIRST_BACK - 1:
                 noise_t = psum.tile([P, P], BF16, name="noise_t", tag="acc5")
                 nc.tensor.transpose(noise_t[:], nz[:], ident[:])
                 nc.scalar.activation(neg_noise[:], noise_t[:, 0:MT], COPY, scale=-1.0)
             if s >= 2:
                 project(s - 2)
-            n_back = BACK_PER_STEP if FIRST_BACK <= s < UNITS else 0
+            n_back = 0 if s < FIRST_BACK or s >= UNITS else BACK_PER_STEP if s < UNITS - 2 else 2
             for pair, g in to_back[:n_back]:
                 back_pair(pair, g, "acc%d" % pair if g == 0 else None)
             to_back = to_back[n_back:]

@@ -85,6 +85,9 @@ def tile_weighted_range_power_step_s13_kernel(
             nc.sync.dma_start(out=b_words[g][:], in_=at_words[g])
 
         nc.scalar.dma_start(out=asc[:], in_=a_scale.rearrange("(k p j) o -> p k (j o)", p=P, j=PACK))
+        warm = keep.tile([P, 2], F32, name="warm")
+        nc.vector.memset(warm[:, 0:1], 0.0)
+        nc.scalar.activation(warm[:, 1:2], warm[:, 0:1], COPY, scale=-1.0)
         nc.vector.memset(b_scales[:].rearrange("p g n -> p (g n)").bitcast(I32), 0)
         nc.gpsimd.memset(nz[:], 0.0)
         make_identity(nc, ident[:])

@@ -20,21 +20,23 @@ COPY = mybir.ActivationFunctionType.Copy
 
 P = 128
 PACK = 4
-KG = M // 512
-NG = N // 512
 S = 512
+KG = M // 512
+NG = N // S
+LAST = NG - 1
+UNITS = NG * KG
+BLOCKS = S // 8
 MT = M // P
 PAIRS = MT // 2
 NACC = 6
-LATE = (6, 7)
-LAST = NG - 1
 
-UNITS = NG * KG
-TENSOR_UNITS = range(0, 13)
-SCALAR_WIDENS = (0, 2, 3, 4, 6, 9, 11)
-BLOCKS = S // 8
 SPANS = (((0,), (1, 2), (3, 4), (5,)), ((0,), (1,), (2, 3), (4, 5)))
 SPAN_OF = {(g, k): span for k in range(KG) for span in SPANS[k % 2] for g in span}
+
+TENSOR_END = 14
+SCALAR_WIDENS = 12
+SHARED_UNITS = 5
+SHARED_BLOCKS = 20
 
 
 def tile_weighted_range_power_step_s13_kernel(
@@ -60,57 +62,53 @@ def tile_weighted_range_power_step_s13_kernel(
         b_words = [keep.tile([P, 2 * M], U8, name="b_words%d" % g, align_bytes=64) for g in range(NG)]
         b_scales = keep.tile([P, NG, M], U8, name="b_scales", align_bytes=64)
         om_rows = keep.tile([P, MT, R], BF16, name="om_rows", align_bytes=64)
-        asc = keep.tile([P, KG, PACK], F32, name="asc")
+        a_sc_first = keep.tile([P, 1, PACK], F32, name="a_sc_first")
+        a_sc_rest = keep.tile([P, KG - 1, PACK], F32, name="a_sc_rest")
         w_sb = keep.tile([P, NG, PACK], BF16, name="w_sb")
-        nz = keep.tile([P, P], BF16, name="nz")
+        noise_rows = keep.tile([P, P], BF16, name="noise_rows")
         ident = keep.tile([P, P], BF16, name="ident")
         neg_noise = keep.tile([P, MT], F32, name="neg_noise")
+        warm = keep.tile([P, 2], F32, name="warm")
 
         a_view = a_bytes.rearrange("(k p j) n -> k p j n", p=P, j=PACK)
+        a_sc_view = a_scale.rearrange("(k p j) o -> p k (j o)", p=P, j=PACK)
         om_view = omega.rearrange("(k p j) r -> k p j r", p=P, j=PACK)
-        scale_view = at_scales.bitcast(I32).rearrange("g q n -> q g n")
+        b_sc_view = at_scales.bitcast(I32).rearrange("g q n -> q g n")
 
         def load_a(g, k, rows=slice(0, PACK)):
-            nc.sync.dma_start(
-                out=a_raw[g, k][:, rows, :], in_=a_view[k][:, rows, S * g : S * (g + len(SPAN_OF[g, k]))]
-            )
+            cols = slice(S * g, S * (g + len(SPAN_OF[g, k])))
+            nc.sync.dma_start(out=a_raw[g, k][:, rows, :], in_=a_view[k][:, rows, cols])
 
         def load_om(k):
             nc.sync.dma_start(out=om_raw[k][:], in_=om_view[k])
 
-        def load_bs(q):
-            nc.sync.dma_start(out=b_scales[q:P:32].bitcast(I32), in_=scale_view[q:16:4])
-
         def load_b(g):
             nc.sync.dma_start(out=b_words[g][:], in_=at_words[g])
 
-        nc.scalar.dma_start(out=asc[:], in_=a_scale.rearrange("(k p j) o -> p k (j o)", p=P, j=PACK))
-        warm = keep.tile([P, 2], F32, name="warm")
+        nc.scalar.dma_start(out=a_sc_first[:], in_=a_sc_view[:, 0:1])
         nc.vector.memset(warm[:, 0:1], 0.0)
         nc.scalar.activation(warm[:, 1:2], warm[:, 0:1], COPY, scale=-1.0)
         nc.vector.memset(b_scales[:].rearrange("p g n -> p (g n)").bitcast(I32), 0)
-        nc.gpsimd.memset(nz[:], 0.0)
+        nc.gpsimd.memset(noise_rows[:], 0.0)
         make_identity(nc, ident[:])
 
         load_a(0, 0, slice(0, 2))
         load_a(0, 0, slice(2, 4))
+        nc.sync.dma_start(out=a_sc_rest[:], in_=a_sc_view[:, 1:KG])
         load_a(0, 1)
         load_a(0, 2)
         load_om(0)
         load_a(0, 3)
-        load_om(1)
-        load_a(1, 0)
-        load_om(2)
-        load_a(1, 1)
-        load_om(3)
-        load_a(1, 2)
+        for k in range(KG - 1):
+            load_om(k + 1)
+            load_a(1, k)
         load_a(1, 3)
         nc.sync.dma_start(out=w_sb[:], in_=sample_w.rearrange("(g p j) -> p g j", p=P, j=PACK))
-        nc.sync.dma_start(out=nz[0:MT, :], in_=noise_var.rearrange("(m p) -> m p", p=P))
+        nc.sync.dma_start(out=noise_rows[0:MT, :], in_=noise_var.rearrange("(m p) -> m p", p=P))
         load_a(2, 1)
         load_a(2, 3)
         for q in range(4):
-            load_bs(q)
+            nc.sync.dma_start(out=b_scales[q:P:32].bitcast(I32), in_=b_sc_view[q:16:4])
         load_b(0)
         load_a(3, 0)
         load_a(3, 2)
@@ -120,23 +118,23 @@ def tile_weighted_range_power_step_s13_kernel(
         load_a(4, 3)
         load_a(5, 0)
         load_a(5, 2)
-        load_b(3)
-        load_b(4)
-        load_b(5)
+        for g in range(3, NG):
+            load_b(g)
         nc.sync.dma_start(out=om_rows[:], in_=omega.rearrange("(m p) r -> p m r", p=P))
 
-        planes, grouped, a_codes, a_scales = {}, {}, {}, {}
-        z, acc, v_grouped, side_by_side = {}, {}, {}, {}
+        planes, side, grouped, a_codes, a_scales = {}, {}, {}, {}, {}
+        om_grouped, z, v_grouped, acc = {}, {}, {}, {}
 
         def widen(g, k, j):
             if j == 0:
                 width = len(SPAN_OF[g, k])
                 planes[g, k] = work.tile([P, PACK, S * width], BF16, name="wide%d" % width, bufs=3 + width, align_bytes=64)
             in_ = a_raw[g, k][:, j, :].bitcast(FP8)
-            if j == PACK - 1 and g * KG + k in SCALAR_WIDENS:
-                nc.scalar.activation(planes[g, k][:, j, :], in_, COPY, scale=asc[:, k, j : j + 1])
+            scale = a_sc_first[:, 0, j : j + 1] if k == 0 else a_sc_rest[:, k - 1, j : j + 1]
+            if j == PACK - 1 and g * KG + k < SCALAR_WIDENS:
+                nc.scalar.activation(planes[g, k][:, j, :], in_, COPY, scale=scale)
             else:
-                nc.vector.tensor_scalar(planes[g, k][:, j, :], in_, asc[:, k, j : j + 1], None, MULT)
+                nc.vector.tensor_scalar(planes[g, k][:, j, :], in_, scale, None, MULT)
 
         def unit_planes(u):
             g, k = divmod(u, KG)
@@ -144,127 +142,118 @@ def tile_weighted_range_power_step_s13_kernel(
             return planes[first, k][:, :, S * (g - first) : S * (g - first + 1)]
 
         def interleave_on_tensor(u):
-            side_by_side[u] = psum.tile([P, S // 2, PACK], BF16, name="side%d" % u, tag="acc%d" % (u % NACC))
+            side[u] = psum.tile([P, S // 2, PACK], BF16, name="side%d" % u, tag="acc%d" % (u % NACC))
             for q in range(2):
                 nc.tensor.matmul(
-                    side_by_side[u][:, P * q : P * (q + 1), :].rearrange("p n j -> p j n"),
+                    side[u][:, P * q : P * (q + 1), :].rearrange("p n j -> p j n"),
                     lhsT=ident[:],
                     rhs=unit_planes(u)[:, :, S // 2 + P * q : S // 2 + P * (q + 1)],
                     start=True,
                     stop=True,
                 )
 
-        def interleave(u, vector_blocks):
-            grouped[u] = work.tile([P, S * PACK], BF16, name="dst_tile", bufs=4, align_bytes=64)
+        def interleave_views(u):
+            grouped[u] = work.tile([P, S * PACK], BF16, name="grouped", bufs=4, align_bytes=64)
             src = unit_planes(u).rearrange("p j (m i t) -> p m t j i", i=2, t=PACK)
             dst = grouped[u][:].rearrange("p (t m i j) -> p m t j i", t=PACK, i=2, j=PACK)
-            cut = BLOCKS // 2 if u in side_by_side else BLOCKS - vector_blocks
-            nc.scalar.copy(dst[:, :cut], src[:, :cut])
-            if u in side_by_side:
-                nc.scalar.copy(
-                    grouped[u][:].rearrange("p (t m j) -> p t m j", t=PACK, j=PACK)[:, :, P // 2 :, :],
-                    side_by_side[u][:].rearrange("p (m t) j -> p t m j", t=PACK),
-                )
-                return None
-            return (dst[:, cut:], src[:, cut:]) if cut < BLOCKS else None
+            return dst, src
 
-        def quantize_a(u):
+        def new_codes(u):
             a_codes[u] = work.tile([P, S], U32, name="codes", bufs=6, align_bytes=64)
             a_scales[u] = work.tile([P, S], U8, name="scales", bufs=6, align_bytes=64)
-            nc.vector.quantize_mx(a_codes[u][:].bitcast(FP8X4), a_scales[u][:], grouped.pop(u)[:])
 
-        def omega_group(k):
-            om_grouped = work.tile([P, R * PACK], BF16, name="om_grouped", bufs=2, align_bytes=64)
+        def quantize_a(u, t0=0, t1=PACK):
+            cols = slice(P * t0, P * t1)
+            nc.vector.quantize_mx(
+                a_codes[u][:, cols].bitcast(FP8X4), a_scales[u][:, cols], grouped[u][:, S * t0 : S * t1]
+            )
+
+        def omega_interleave(k):
+            om_grouped[k] = work.tile([P, R * PACK], BF16, name="om_grouped", bufs=2, align_bytes=64)
             nc.vector.tensor_copy(
-                om_grouped[:].rearrange("p (c i j) -> p c j i", i=2, j=PACK),
+                om_grouped[k][:].rearrange("p (c i j) -> p c j i", i=2, j=PACK),
                 om_raw[k][:].rearrange("p j (c i) -> p c j i", i=2),
             )
-            return om_grouped
 
-        def omega_quantize(k, om_grouped):
-            nc.vector.quantize_mx(om_codes[k][:].bitcast(FP8X4), om_scales[k][:], om_grouped[:])
+        def omega_quantize(k):
+            nc.vector.quantize_mx(om_codes[k][:].bitcast(FP8X4), om_scales[k][:], om_grouped[k][:])
 
-        def project(u):
+        def project(u, ts=range(PACK), closing_t=PACK - 1):
             g, k = divmod(u, KG)
-            codes, scales = a_codes.pop(u), a_scales.pop(u)
             for h in range(2):
                 if k == 0:
                     z[g, h] = psum.tile([P, PACK, P], F32, name="z%d_%d" % (g, h), tag="z%d" % h)
-                for t in range(PACK):
+                for t in ts:
                     nc.tensor.matmul_mx(
                         out=z[g, h][:, t, :],
-                        lhsT=codes[:, P * t : P * (t + 1)].bitcast(FP8X4),
-                        lhsT_scale=scales[:, P * t : P * (t + 1)],
+                        lhsT=a_codes[u][:, P * t : P * (t + 1)].bitcast(FP8X4),
+                        lhsT_scale=a_scales[u][:, P * t : P * (t + 1)],
                         rhs=om_codes[k][:, P * h : P * (h + 1)].bitcast(FP8X4),
                         rhs_scale=om_scales[k][:, P * h : P * (h + 1)],
                         start=(k == 0 and t == 0),
-                        stop=(k == KG - 1 and t == PACK - 1),
+                        stop=(k == KG - 1 and t == closing_t),
                     )
 
-        HALF = P * PACK
-
         def weigh(g):
-            v_grouped[g] = work.tile([P, R * PACK], BF16, name="v_grouped", bufs=2, align_bytes=64)
+            v_grouped[g] = work.tile([P, 2, P * PACK], BF16, name="v_grouped", bufs=2, align_bytes=64)
             for h in range(2):
                 nc.vector.tensor_tensor(
-                    v_grouped[g][:, HALF * h : HALF * (h + 1)].rearrange("p (c i j) -> p c j i", i=2, j=PACK),
-                    z[g, h][:].rearrange("p j (c i) -> p c j i", i=2),
+                    v_grouped[g][:, h, :].rearrange("p (c i t) -> p c t i", i=2, t=PACK),
+                    z[g, h][:].rearrange("p t (c i) -> p c t i", i=2),
                     w_sb[:, g : g + 1, :].unsqueeze(3).to_broadcast([P, P // 2, PACK, 2]),
                     MULT,
                 )
 
-        def quantize_v(g, pieces):
-            width = R // pieces
-            for i in range(pieces):
-                cols = slice(width * i, width * (i + 1))
-                nc.vector.quantize_mx(
-                    v_codes[g][:, cols].bitcast(FP8X4),
-                    v_scales[g][:, cols],
-                    v_grouped[g][:, PACK * width * i : PACK * width * (i + 1)],
-                )
-
-        def back(pair, g, i, h, first, last):
-            m = 2 * pair + i
-            nc.tensor.matmul_mx(
-                out=acc[pair][:, i, P * h : P * (h + 1)],
-                lhsT=b_words[g][:, 2 * P * m : 2 * P * (m + 1)].bitcast(FP4X4),
-                lhsT_scale=b_scales[:, g, P * m : P * (m + 1)],
-                rhs=v_codes[g][:, P * h : P * (h + 1)].bitcast(FP8X4),
-                rhs_scale=v_scales[g][:, P * h : P * (h + 1)],
-                start=first,
-                stop=last,
+        def quantize_v(g, h0=0, h1=2):
+            cols = slice(P * h0, P * h1)
+            nc.vector.quantize_mx(
+                v_codes[g][:, cols].bitcast(FP8X4),
+                v_scales[g][:, cols],
+                v_grouped[g][:, h0:h1, :].rearrange("p h c -> p (h c)"),
             )
 
-        def back_pair(pair, g, tag=None):
-            if tag is not None:
-                acc[pair] = psum.tile([P, 2, R], F32, name="acc%d_%d" % (pair, g), tag=tag)
-            closes = g == LAST
+        def back(pair, g):
+            if g == 0:
+                tag = "acc%d" % pair if pair < NACC else "z%d" % (pair - NACC)
+                acc[pair] = psum.tile([P, 2, R], F32, name="acc%d" % pair, tag=tag)
             for h in range(2):
                 for i in range(2):
-                    back(pair, g, i, h, tag is not None and h == 0 and i == 0, closes and h == 1 and i == 1)
+                    m = 2 * pair + i
+                    nc.tensor.matmul_mx(
+                        out=acc[pair][:, i, P * h : P * (h + 1)],
+                        lhsT=b_words[g][:, 2 * P * m : 2 * P * (m + 1)].bitcast(FP4X4),
+                        lhsT_scale=b_scales[:, g, P * m : P * (m + 1)],
+                        rhs=v_codes[g][:, P * h : P * (h + 1)].bitcast(FP8X4),
+                        rhs_scale=v_scales[g][:, P * h : P * (h + 1)],
+                        start=(g == 0 and h == 0 and i == 0),
+                        stop=(g == LAST and h == 1 and i == 1),
+                    )
+
+        def noise_onto_partitions():
+            noise_t = psum.tile([P, P], BF16, name="noise_t", tag="acc%d" % (NACC - 1))
+            nc.tensor.transpose(noise_t[:], noise_rows[:], ident[:])
+            nc.scalar.activation(neg_noise[:], noise_t[:, 0:MT], COPY, scale=-1.0)
 
         out_view = out.rearrange("(b i p) r -> b p i r", i=2, p=P)
-        y = {}
-
-        def subtract(m, result):
-            nc.vector.scalar_tensor_tensor(
-                result, om_rows[:, m, :], neg_noise[:, m : m + 1], acc[m // 2][:, m % 2, :], MULT, ADD
-            )
 
         def finish(pair):
-            y[pair] = work.tile([P, 2, R], F32, name="y", bufs=8)
+            y = work.tile([P, 2, R], F32, name="y", bufs=PAIRS)
             for i in range(2):
                 m = 2 * pair + i
-                subtract(m, y[pair][:, i, :])
-            nc.sync.dma_start(out=out_view[pair], in_=y[pair][:])
+                nc.vector.scalar_tensor_tensor(
+                    y[:, i, :], om_rows[:, m, :], neg_noise[:, m : m + 1], acc[pair][:, i, :], MULT, ADD
+                )
+                if pair == PAIRS - 1:
+                    nc.sync.dma_start(out=out_view[pair][:, i, :], in_=y[:, i, :])
+            if pair < PAIRS - 1:
+                nc.sync.dma_start(out=out_view[pair], in_=y[:])
 
         AHEAD = 2
-        SHARED_UNITS = 6
-        SHARED_BLOCKS = 16
-        FIRST_BACK = 13
         BACK_PER_STEP = 3
         LATE_EARLY = 3
         to_widen = [(g, k, j) for g in range(NG) for k in range(KG) if SPAN_OF[g, k][0] == g for j in range(PACK)]
+        to_project = list(range(UNITS))
+        to_back = []
 
         def widen_for(u):
             while to_widen:
@@ -274,51 +263,78 @@ def tile_weighted_range_power_step_s13_kernel(
                     break
                 widen(*to_widen.pop(0))
 
-        to_back = []
-        om_grouped = {}
+        def weigh_step(g):
+            step = KG * (g + 1) + AHEAD
+            return step + 1 if step <= TENSOR_END else step
+
         widen_for(AHEAD - 1)
-        interleave_on_tensor(0)
-        for s in range(UNITS + 2):
-            left = interleave(s, SHARED_BLOCKS if s >= UNITS - SHARED_UNITS else 0) if s < UNITS else None
-            ready = [s // KG - 1] if s % KG == 2 and s > KG else []
+        interleave_on_tensor(1)
+        for s in range(UNITS - 1):
+            dst, src = interleave_views(s)
+            cut = BLOCKS // 2 if s in side else BLOCKS - SHARED_BLOCKS if s >= UNITS - SHARED_UNITS else BLOCKS
+            nc.scalar.copy(dst[:, :cut], src[:, :cut])
+            if s in side:
+                nc.scalar.copy(
+                    grouped[s][:].rearrange("p (t m j) -> p t m j", t=PACK, j=PACK)[:, :, P // 2 :, :],
+                    side[s][:].rearrange("p (m t) j -> p t m j", t=PACK),
+                )
+            ready = [g for g in range(LAST) if weigh_step(g) == s]
             if 1 <= s <= KG:
-                om_grouped[s - 1] = omega_group(s - 1)
-            if s >= 2:
-                quantize_a(s - 2)
+                omega_interleave(s - 1)
+            if s >= AHEAD:
+                new_codes(s - AHEAD)
+                quantize_a(s - AHEAD)
             for g in ready:
                 weigh(g)
             widen_for(s + AHEAD)
-            if left is not None:
-                nc.vector.tensor_copy(*left)
+            if s not in side and cut < BLOCKS:
+                nc.vector.tensor_copy(dst[:, cut:], src[:, cut:])
             if 1 <= s <= KG:
-                omega_quantize(s - 1, om_grouped[s - 1])
+                omega_quantize(s - 1)
             for g in ready:
-                quantize_v(g, 1)
-                to_back += [(pair, g) for pair in range(NACC)]
-            if s + 1 in TENSOR_UNITS:
-                interleave_on_tensor(s + 1)
-            if s == FIRST_BACK - 1:
-                noise_t = psum.tile([P, P], BF16, name="noise_t", tag="acc5")
-                nc.tensor.transpose(noise_t[:], nz[:], ident[:])
-                nc.scalar.activation(neg_noise[:], noise_t[:, 0:MT], COPY, scale=-1.0)
-            if s >= 2:
-                project(s - 2)
-            n_back = 0 if s < FIRST_BACK or s >= UNITS else BACK_PER_STEP if s < UNITS - 2 else 2
-            for pair, g in to_back[:n_back]:
-                back_pair(pair, g, "acc%d" % pair if g == 0 else None)
-            to_back = to_back[n_back:]
+                quantize_v(g)
+                to_back.extend((pair, g) for pair in range(NACC))
+            if s == TENSOR_END - 1:
+                noise_onto_partitions()
+            while to_project[0] <= s - AHEAD and to_project[0] // KG <= len(v_grouped):
+                project(to_project.pop(0))
+            if s + AHEAD < TENSOR_END:
+                interleave_on_tensor(s + AHEAD)
+            if s >= TENSOR_END:
+                for item in to_back[: BACK_PER_STEP if s < UNITS - 2 else 2]:
+                    back(*item)
+                    to_back.remove(item)
 
-        for pair, g in to_back:
-            back_pair(pair, g)
+        u = UNITS - 1
+        dst, src = interleave_views(u)
+        nc.scalar.copy(dst[:, :, 0:2], src[:, :, 0:2])
+        nc.scalar.copy(dst[:, :, 2:3], src[:, :, 2:3])
+        new_codes(u - 2)
+        quantize_a(u - 2)
+        project(u - 2)
+        for item in to_back[:2]:
+            back(*item)
+        nc.vector.tensor_copy(dst[:, :, 3:4], src[:, :, 3:4])
+        new_codes(u - 1)
+        quantize_a(u - 1)
+        project(u - 1)
+        new_codes(u)
+        for t0, t1 in ((3, 4), (0, 2), (2, 3)):
+            quantize_a(u, t0, t1)
+            project(u, range(t0, t1), closing_t=2)
+        for item in to_back[2:]:
+            back(*item)
+
         weigh(LAST)
-        quantize_v(LAST, 2)
-        late = [(pair, g) for pair in LATE for g in range(NG)]
-        for pair, g in late[:LATE_EARLY]:
-            back_pair(pair, g, "z%d" % (pair - NACC) if g == 0 else None)
+        for h in range(2):
+            quantize_v(LAST, h, h + 1)
+        late = [(pair, g) for pair in range(NACC, PAIRS) for g in range(NG)]
+        for item in late[:LATE_EARLY]:
+            back(*item)
         for pair in range(NACC):
-            back_pair(pair, LAST)
+            back(pair, LAST)
             finish(pair)
         for pair, g in late[LATE_EARLY:]:
-            back_pair(pair, g, "z%d" % (pair - NACC) if g == 0 else None)
+            back(pair, g)
             if g == LAST:
                 finish(pair)

@@ -36,7 +36,8 @@ SPAN_OF = {(g, k): span for k in range(KG) for span in SPANS[k % 2] for g in spa
 TENSOR_END = 14
 SCALAR_WIDENS = 12
 SHARED_UNITS = 5
-SHARED_BLOCKS = 20
+THIRD_EVERY = 2
+SHARED_BLOCKS = 16
 
 
 def tile_weighted_range_power_step_s13_kernel(
@@ -123,7 +124,7 @@ def tile_weighted_range_power_step_s13_kernel(
         nc.sync.dma_start(out=om_rows[:], in_=omega.rearrange("(m p) r -> p m r", p=P))
 
         planes, side, grouped, a_codes, a_scales = {}, {}, {}, {}, {}
-        om_grouped, z, v_grouped, acc = {}, {}, {}, {}
+        om_grouped, z, v_grouped, acc, y = {}, {}, {}, {}, {}
 
         def widen(g, k, j):
             if j == 0:
@@ -142,15 +143,19 @@ def tile_weighted_range_power_step_s13_kernel(
             return planes[first, k][:, :, S * (g - first) : S * (g - first + 1)]
 
         def interleave_on_tensor(u):
-            side[u] = psum.tile([P, S // 2, PACK], BF16, name="side%d" % u, tag="acc%d" % (u % NACC))
-            for q in range(2):
-                nc.tensor.matmul(
-                    side[u][:, P * q : P * (q + 1), :].rearrange("p n j -> p j n"),
-                    lhsT=ident[:],
-                    rhs=unit_planes(u)[:, :, S // 2 + P * q : S // 2 + P * (q + 1)],
-                    start=True,
-                    stop=True,
-                )
+            side[u] = []
+            for q0, q1 in ((2, 4), (1, 2)) if u % THIRD_EVERY == 0 else ((2, 4),):
+                bank = psum.tile([P, P * (q1 - q0), PACK], BF16, name="side", tag="acc%d" % (len(banks) % NACC))
+                banks.append(bank)
+                side[u].append((q0, q1, bank))
+                for q in range(q0, q1):
+                    nc.tensor.matmul(
+                        bank[:, P * (q - q0) : P * (q - q0 + 1), :].rearrange("p n j -> p j n"),
+                        lhsT=ident[:],
+                        rhs=unit_planes(u)[:, :, P * q : P * (q + 1)],
+                        start=True,
+                        stop=True,
+                    )
 
         def interleave_views(u):
             grouped[u] = work.tile([P, S * PACK], BF16, name="grouped", bufs=4, align_bytes=64)
@@ -236,24 +241,27 @@ def tile_weighted_range_power_step_s13_kernel(
 
         out_view = out.rearrange("(b i p) r -> b p i r", i=2, p=P)
 
-        def finish(pair):
-            y = work.tile([P, 2, R], F32, name="y", bufs=PAIRS)
+        def noise_term(pair):
+            y[pair] = work.tile([P, 2, R], F32, name="y", bufs=PAIRS)
             for i in range(2):
                 m = 2 * pair + i
-                nc.vector.scalar_tensor_tensor(
-                    y[:, i, :], om_rows[:, m, :], neg_noise[:, m : m + 1], acc[pair][:, i, :], MULT, ADD
-                )
-                if pair == PAIRS - 1:
-                    nc.sync.dma_start(out=out_view[pair][:, i, :], in_=y[:, i, :])
-            if pair < PAIRS - 1:
-                nc.sync.dma_start(out=out_view[pair], in_=y[:])
+                nc.scalar.activation(y[pair][:, i, :], om_rows[:, m, :], COPY, scale=neg_noise[:, m : m + 1])
+
+        def finish(pair):
+            for part in [slice(0, 2)] if pair < PAIRS - 1 else [slice(0, 1), slice(1, 2)]:
+                nc.vector.tensor_tensor(y[pair][:, part, :], acc[pair][:, part, :], y[pair][:, part, :], ADD)
+                nc.sync.dma_start(out=out_view[pair][:, part, :], in_=y[pair][:, part, :])
 
         AHEAD = 2
         BACK_PER_STEP = 3
         LATE_EARLY = 3
+        BACK_A = 1
+        BACK_B = 1
+        BACK_C = 1
         to_widen = [(g, k, j) for g in range(NG) for k in range(KG) if SPAN_OF[g, k][0] == g for j in range(PACK)]
         to_project = list(range(UNITS))
         to_back = []
+        banks = []
 
         def widen_for(u):
             while to_widen:
@@ -269,14 +277,14 @@ def tile_weighted_range_power_step_s13_kernel(
 
         widen_for(AHEAD - 1)
         interleave_on_tensor(1)
-        for s in range(UNITS - 1):
+        for s in range(UNITS - KG):
             dst, src = interleave_views(s)
-            cut = BLOCKS // 2 if s in side else BLOCKS - SHARED_BLOCKS if s >= UNITS - SHARED_UNITS else BLOCKS
+            cut = BLOCKS // 4 * side[s][-1][0] if s in side else BLOCKS - SHARED_BLOCKS if s >= UNITS - SHARED_UNITS else BLOCKS
             nc.scalar.copy(dst[:, :cut], src[:, :cut])
-            if s in side:
+            for q0, q1, bank in side.get(s, ()):
                 nc.scalar.copy(
-                    grouped[s][:].rearrange("p (t m j) -> p t m j", t=PACK, j=PACK)[:, :, P // 2 :, :],
-                    side[s][:].rearrange("p (m t) j -> p t m j", t=PACK),
+                    grouped[s][:].rearrange("p (t m j) -> p t m j", t=PACK, j=PACK)[:, :, 32 * q0 : 32 * q1, :],
+                    bank[:].rearrange("p (m t) j -> p t m j", t=PACK),
                 )
             ready = [g for g in range(LAST) if weigh_step(g) == s]
             if 1 <= s <= KG:
@@ -301,28 +309,63 @@ def tile_weighted_range_power_step_s13_kernel(
             if s + AHEAD < TENSOR_END:
                 interleave_on_tensor(s + AHEAD)
             if s >= TENSOR_END:
-                for item in to_back[: BACK_PER_STEP if s < UNITS - 2 else 2]:
+                for item in to_back[:BACK_PER_STEP]:
                     back(*item)
                     to_back.remove(item)
+
+        first = UNITS - KG
+        cut = BLOCKS - SHARED_BLOCKS
+        views = {}
+
+        def scalar_share(u):
+            views[u] = interleave_views(u)
+            nc.scalar.copy(views[u][0][:, :cut], views[u][1][:, :cut])
+
+        def vector_share(u):
+            nc.vector.tensor_copy(views[u][0][:, cut:], views[u][1][:, cut:])
+
+        def quantize_and_project(u, n_back):
+            new_codes(u)
+            quantize_a(u)
+            project(u)
+            for item in to_back[:n_back]:
+                back(*item)
+                to_back.remove(item)
+
+        scalar_share(first)
+        quantize_and_project(first - 2, 0)
+        for item in to_widen[:2]:
+            widen(*item)
+        quantize_and_project(first - 1, NACC)
+        for item in to_widen[2:]:
+            widen(*item)
+        vector_share(first)
+        weigh(LAST - 1)
+        scalar_share(first + 1)
+        vector_share(first + 1)
+        quantize_v(LAST - 1)
+        to_back.extend((pair, LAST - 1) for pair in range(NACC))
+        for item in to_back[:BACK_A]:
+            back(*item)
+            to_back.remove(item)
+        quantize_and_project(first, BACK_B)
+        scalar_share(first + 2)
+        vector_share(first + 2)
+        quantize_and_project(first + 1, BACK_C)
 
         u = UNITS - 1
         dst, src = interleave_views(u)
         nc.scalar.copy(dst[:, :, 0:2], src[:, :, 0:2])
         nc.scalar.copy(dst[:, :, 2:3], src[:, :, 2:3])
-        new_codes(u - 2)
-        quantize_a(u - 2)
-        project(u - 2)
-        for item in to_back[:2]:
-            back(*item)
+        for pair in range(PAIRS):
+            noise_term(pair)
         nc.vector.tensor_copy(dst[:, :, 3:4], src[:, :, 3:4])
-        new_codes(u - 1)
-        quantize_a(u - 1)
-        project(u - 1)
+        quantize_and_project(u - 1, 0)
         new_codes(u)
         for t0, t1 in ((3, 4), (0, 2), (2, 3)):
             quantize_a(u, t0, t1)
             project(u, range(t0, t1), closing_t=2)
-        for item in to_back[2:]:
+        for item in to_back:
             back(*item)
 
         weigh(LAST)

@@ -34,9 +34,8 @@ SPANS = (((0,), (1, 2), (3, 4), (5,)), ((0,), (1,), (2, 3), (4, 5)))
 SPAN_OF = {(g, k): span for k in range(KG) for span in SPANS[k % 2] for g in span}
 
 TENSOR_END = 14
-SCALAR_WIDENS = 12
+SCALAR_WIDENS = 10
 SHARED_UNITS = 5
-THIRD_EVERY = 2
 SHARED_BLOCKS = 16
 
 
@@ -87,6 +86,7 @@ def tile_weighted_range_power_step_s13_kernel(
             nc.sync.dma_start(out=b_words[g][:], in_=at_words[g])
 
         nc.scalar.dma_start(out=a_sc_first[:], in_=a_sc_view[:, 0:1])
+        nc.scalar.dma_start(out=a_sc_rest[:], in_=a_sc_view[:, 1:KG])
         nc.vector.memset(warm[:, 0:1], 0.0)
         nc.scalar.activation(warm[:, 1:2], warm[:, 0:1], COPY, scale=-1.0)
         nc.vector.memset(b_scales[:].rearrange("p g n -> p (g n)").bitcast(I32), 0)
@@ -95,14 +95,13 @@ def tile_weighted_range_power_step_s13_kernel(
 
         load_a(0, 0, slice(0, 2))
         load_a(0, 0, slice(2, 4))
-        nc.sync.dma_start(out=a_sc_rest[:], in_=a_sc_view[:, 1:KG])
         load_a(0, 1)
         load_a(0, 2)
         load_om(0)
         load_a(0, 3)
         for k in range(KG - 1):
-            load_om(k + 1)
             load_a(1, k)
+            load_om(k + 1)
         load_a(1, 3)
         nc.sync.dma_start(out=w_sb[:], in_=sample_w.rearrange("(g p j) -> p g j", p=P, j=PACK))
         nc.sync.dma_start(out=noise_rows[0:MT, :], in_=noise_var.rearrange("(m p) -> m p", p=P))
@@ -143,19 +142,15 @@ def tile_weighted_range_power_step_s13_kernel(
             return planes[first, k][:, :, S * (g - first) : S * (g - first + 1)]
 
         def interleave_on_tensor(u):
-            side[u] = []
-            for q0, q1 in ((2, 4), (1, 2)) if u % THIRD_EVERY == 0 else ((2, 4),):
-                bank = psum.tile([P, P * (q1 - q0), PACK], BF16, name="side", tag="acc%d" % (len(banks) % NACC))
-                banks.append(bank)
-                side[u].append((q0, q1, bank))
-                for q in range(q0, q1):
-                    nc.tensor.matmul(
-                        bank[:, P * (q - q0) : P * (q - q0 + 1), :].rearrange("p n j -> p j n"),
-                        lhsT=ident[:],
-                        rhs=unit_planes(u)[:, :, P * q : P * (q + 1)],
-                        start=True,
-                        stop=True,
-                    )
+            side[u] = psum.tile([P, S // 2, PACK], BF16, name="side%d" % u, tag="acc%d" % (u % NACC))
+            for q in range(2):
+                nc.tensor.matmul(
+                    side[u][:, P * q : P * (q + 1), :].rearrange("p n j -> p j n"),
+                    lhsT=ident[:],
+                    rhs=unit_planes(u)[:, :, S // 2 + P * q : S // 2 + P * (q + 1)],
+                    start=True,
+                    stop=True,
+                )
 
         def interleave_views(u):
             grouped[u] = work.tile([P, S * PACK], BF16, name="grouped", bufs=4, align_bytes=64)
@@ -261,7 +256,6 @@ def tile_weighted_range_power_step_s13_kernel(
         to_widen = [(g, k, j) for g in range(NG) for k in range(KG) if SPAN_OF[g, k][0] == g for j in range(PACK)]
         to_project = list(range(UNITS))
         to_back = []
-        banks = []
 
         def widen_for(u):
             while to_widen:
@@ -279,12 +273,12 @@ def tile_weighted_range_power_step_s13_kernel(
         interleave_on_tensor(1)
         for s in range(UNITS - KG):
             dst, src = interleave_views(s)
-            cut = BLOCKS // 4 * side[s][-1][0] if s in side else BLOCKS - SHARED_BLOCKS if s >= UNITS - SHARED_UNITS else BLOCKS
+            cut = BLOCKS // 2 if s in side else BLOCKS - SHARED_BLOCKS if s >= UNITS - SHARED_UNITS else BLOCKS
             nc.scalar.copy(dst[:, :cut], src[:, :cut])
-            for q0, q1, bank in side.get(s, ()):
+            if s in side:
                 nc.scalar.copy(
-                    grouped[s][:].rearrange("p (t m j) -> p t m j", t=PACK, j=PACK)[:, :, 32 * q0 : 32 * q1, :],
-                    bank[:].rearrange("p (m t) j -> p t m j", t=PACK),
+                    grouped[s][:].rearrange("p (t m j) -> p t m j", t=PACK, j=PACK)[:, :, P // 2 :, :],
+                    side[s][:].rearrange("p (m t) j -> p t m j", t=PACK),
                 )
             ready = [g for g in range(LAST) if weigh_step(g) == s]
             if 1 <= s <= KG:

@@ -93,6 +93,12 @@ def tile_weighted_range_power_step_s13_kernel(
         nc.gpsimd.memset(noise_rows[:], 0.0)
         make_identity(nc, ident[:])
 
+        warm_bank = psum.tile([P, PACK, P], F32, name="warm_bank", tag="z0")
+        for i in range(3):
+            nc.tensor.matmul(
+                warm_bank[:], lhsT=ident[:], rhs=ident[:].unsqueeze(1).to_broadcast([P, PACK, P]), start=True, stop=True
+            )
+
         load_a(0, 0, slice(0, 2))
         load_a(0, 0, slice(2, 4))
         load_a(0, 1)
@@ -270,7 +276,8 @@ def tile_weighted_range_power_step_s13_kernel(
             return step + 1 if step <= TENSOR_END else step
 
         widen_for(AHEAD - 1)
-        interleave_on_tensor(1)
+        for u in range(AHEAD):
+            interleave_on_tensor(u)
         for s in range(UNITS - KG):
             dst, src = interleave_views(s)
             cut = BLOCKS // 2 if s in side else BLOCKS - SHARED_BLOCKS if s >= UNITS - SHARED_UNITS else BLOCKS

@@ -34,7 +34,7 @@ SPANS = (((0,), (1, 2), (3, 4), (5,)), ((0,), (1,), (2, 3), (4, 5)))
 SPAN_OF = {(g, k): span for k in range(KG) for span in SPANS[k % 2] for g in span}
 
 TENSOR_END = 14
-SCALAR_WIDENS = 10
+SCALAR_WIDENS = 12
 SHARED_UNITS = 5
 SHARED_BLOCKS = 16
 
@@ -148,15 +148,19 @@ def tile_weighted_range_power_step_s13_kernel(
             return planes[first, k][:, :, S * (g - first) : S * (g - first + 1)]
 
         def interleave_on_tensor(u):
-            side[u] = psum.tile([P, S // 2, PACK], BF16, name="side%d" % u, tag="acc%d" % (u % NACC))
-            for q in range(2):
-                nc.tensor.matmul(
-                    side[u][:, P * q : P * (q + 1), :].rearrange("p n j -> p j n"),
-                    lhsT=ident[:],
-                    rhs=unit_planes(u)[:, :, S // 2 + P * q : S // 2 + P * (q + 1)],
-                    start=True,
-                    stop=True,
-                )
+            side[u] = []
+            for q0, q1 in ((2, 4), (1, 2)) if u % KG == 2 else ((2, 4),):
+                bank = psum.tile([P, P * (q1 - q0), PACK], BF16, name="side", tag="acc%d" % (len(banks) % NACC))
+                banks.append(bank)
+                side[u].append((q0, q1, bank))
+                for q in range(q0, q1):
+                    nc.tensor.matmul(
+                        bank[:, P * (q - q0) : P * (q - q0 + 1), :].rearrange("p n j -> p j n"),
+                        lhsT=ident[:],
+                        rhs=unit_planes(u)[:, :, P * q : P * (q + 1)],
+                        start=True,
+                        stop=True,
+                    )
 
         def interleave_views(u):
             grouped[u] = work.tile([P, S * PACK], BF16, name="grouped", bufs=4, align_bytes=64)
@@ -262,6 +266,7 @@ def tile_weighted_range_power_step_s13_kernel(
         to_widen = [(g, k, j) for g in range(NG) for k in range(KG) if SPAN_OF[g, k][0] == g for j in range(PACK)]
         to_project = list(range(UNITS))
         to_back = []
+        banks = []
 
         def widen_for(u):
             while to_widen:
@@ -280,12 +285,12 @@ def tile_weighted_range_power_step_s13_kernel(
             interleave_on_tensor(u)
         for s in range(UNITS - KG):
             dst, src = interleave_views(s)
-            cut = BLOCKS // 2 if s in side else BLOCKS - SHARED_BLOCKS if s >= UNITS - SHARED_UNITS else BLOCKS
+            cut = BLOCKS // 4 * side[s][-1][0] if s in side else BLOCKS - SHARED_BLOCKS if s >= UNITS - SHARED_UNITS else BLOCKS
             nc.scalar.copy(dst[:, :cut], src[:, :cut])
-            if s in side:
+            for q0, q1, bank in side.get(s, ()):
                 nc.scalar.copy(
-                    grouped[s][:].rearrange("p (t m j) -> p t m j", t=PACK, j=PACK)[:, :, P // 2 :, :],
-                    side[s][:].rearrange("p (m t) j -> p t m j", t=PACK),
+                    grouped[s][:].rearrange("p (t m j) -> p t m j", t=PACK, j=PACK)[:, :, 32 * q0 : 32 * q1, :],
+                    bank[:].rearrange("p (m t) j -> p t m j", t=PACK),
                 )
             ready = [g for g in range(LAST) if weigh_step(g) == s]
             if 1 <= s <= KG:

@@ -93,12 +93,6 @@ def tile_weighted_range_power_step_s13_kernel(
         nc.gpsimd.memset(noise_rows[:], 0.0)
         make_identity(nc, ident[:])
 
-        warm_bank = psum.tile([P, PACK, P], F32, name="warm_bank", tag="z0")
-        for i in range(3):
-            nc.tensor.matmul(
-                warm_bank[:], lhsT=ident[:], rhs=ident[:].unsqueeze(1).to_broadcast([P, PACK, P]), start=True, stop=True
-            )
-
         load_a(0, 0, slice(0, 2))
         load_a(0, 0, slice(2, 4))
         load_a(0, 1)

@@ -26,17 +26,24 @@ NG = N // S
 LAST = NG - 1
 UNITS = NG * KG
 BLOCKS = S // 8
+QUARTER = BLOCKS // 4
 MT = M // P
-PAIRS = MT // 2
+
 NACC = 6
+RESIDENT = [(2 * b, 2 * b + 1) for b in range(NACC)]
+LATE = [(12, 13), (14,), (15,)]
+BANK_OF = dict([(tiles, "acc%d" % b) for b, tiles in enumerate(RESIDENT)] + list(zip(LATE, ("z0", "z1", "acc0"))))
 
 SPANS = (((0,), (1, 2), (3, 4), (5,)), ((0,), (1,), (2, 3), (4, 5)))
 SPAN_OF = {(g, k): span for k in range(KG) for span in SPANS[k % 2] for g in span}
 
 TENSOR_END = 14
+THREE_QUARTER_PASS = 2
 SCALAR_WIDENS = 12
 SHARED_UNITS = 5
-SHARED_BLOCKS = 16
+AHEAD = 2
+BACK_PER_STEP = 3 * NACC // (UNITS - KG - TENSOR_END)
+LATE_EARLY = 3
 
 
 def tile_weighted_range_power_step_s13_kernel(
@@ -93,9 +100,9 @@ def tile_weighted_range_power_step_s13_kernel(
         nc.gpsimd.memset(noise_rows[:], 0.0)
         make_identity(nc, ident[:])
 
-        load_a(0, 0, slice(0, 2))
-        load_a(0, 0, slice(2, 4))
-        load_a(0, 1)
+        for k in range(2):
+            load_a(0, k, slice(0, 2))
+            load_a(0, k, slice(2, 4))
         load_a(0, 2)
         load_om(0)
         load_a(0, 3)
@@ -128,7 +135,9 @@ def tile_weighted_range_power_step_s13_kernel(
         def widen(g, k, j):
             if j == 0:
                 width = len(SPAN_OF[g, k])
-                planes[g, k] = work.tile([P, PACK, S * width], BF16, name="wide%d" % width, bufs=3 + width, align_bytes=64)
+                planes[g, k] = work.tile(
+                    [P, PACK, S * width], BF16, name="wide%d" % width, bufs=3 + width, align_bytes=64
+                )
             in_ = a_raw[g, k][:, j, :].bitcast(FP8)
             scale = a_sc_first[:, 0, j : j + 1] if k == 0 else a_sc_rest[:, k - 1, j : j + 1]
             if j == PACK - 1 and g * KG + k < SCALAR_WIDENS:
@@ -143,7 +152,7 @@ def tile_weighted_range_power_step_s13_kernel(
 
         def interleave_on_tensor(u):
             side[u] = []
-            for q0, q1 in ((2, 4), (1, 2)) if u % KG == 2 else ((2, 4),):
+            for q0, q1 in ((2, 4), (1, 2)) if u % KG == THREE_QUARTER_PASS else ((2, 4),):
                 bank = psum.tile([P, P * (q1 - q0), PACK], BF16, name="side", tag="acc%d" % (len(banks) % NACC))
                 banks.append(bank)
                 side[u].append((q0, q1, bank))
@@ -157,7 +166,7 @@ def tile_weighted_range_power_step_s13_kernel(
                     )
 
         def interleave_views(u):
-            grouped[u] = work.tile([P, S * PACK], BF16, name="grouped", bufs=4, align_bytes=64)
+            grouped[u] = work.tile([P, S * PACK], BF16, name="grouped", bufs=AHEAD + 2, align_bytes=64)
             src = unit_planes(u).rearrange("p j (m i t) -> p m t j i", i=2, t=PACK)
             dst = grouped[u][:].rearrange("p (t m i j) -> p m t j i", t=PACK, i=2, j=PACK)
             return dst, src
@@ -182,9 +191,9 @@ def tile_weighted_range_power_step_s13_kernel(
         def omega_quantize(k):
             nc.vector.quantize_mx(om_codes[k][:].bitcast(FP8X4), om_scales[k][:], om_grouped[k][:])
 
-        def project(u, ts=range(PACK), closing_t=PACK - 1):
+        def project(u, ts=range(PACK), closing_t=PACK - 1, halves=range(2)):
             g, k = divmod(u, KG)
-            for h in range(2):
+            for h in halves:
                 if k == 0:
                     z[g, h] = psum.tile([P, PACK, P], F32, name="z%d_%d" % (g, h), tag="z%d" % h)
                 for t in ts:
@@ -216,47 +225,40 @@ def tile_weighted_range_power_step_s13_kernel(
                 v_grouped[g][:, h0:h1, :].rearrange("p h c -> p (h c)"),
             )
 
-        def back(pair, g):
+        def back(tiles, g):
             if g == 0:
-                tag = "acc%d" % pair if pair < NACC else "z%d" % (pair - NACC)
-                acc[pair] = psum.tile([P, 2, R], F32, name="acc%d" % pair, tag=tag)
+                acc[tiles] = psum.tile([P, len(tiles), R], F32, name="acc%d" % tiles[0], tag=BANK_OF[tiles])
             for h in range(2):
-                for i in range(2):
-                    m = 2 * pair + i
+                for i, m in enumerate(tiles):
                     nc.tensor.matmul_mx(
-                        out=acc[pair][:, i, P * h : P * (h + 1)],
+                        out=acc[tiles][:, i, P * h : P * (h + 1)],
                         lhsT=b_words[g][:, 2 * P * m : 2 * P * (m + 1)].bitcast(FP4X4),
                         lhsT_scale=b_scales[:, g, P * m : P * (m + 1)],
                         rhs=v_codes[g][:, P * h : P * (h + 1)].bitcast(FP8X4),
                         rhs_scale=v_scales[g][:, P * h : P * (h + 1)],
                         start=(g == 0 and h == 0 and i == 0),
-                        stop=(g == LAST and h == 1 and i == 1),
+                        stop=(g == LAST and h == 1 and i == len(tiles) - 1),
                     )
 
         def noise_onto_partitions():
             noise_t = psum.tile([P, P], BF16, name="noise_t", tag="acc%d" % (NACC - 1))
             nc.tensor.transpose(noise_t[:], noise_rows[:], ident[:])
-            nc.scalar.activation(neg_noise[:], noise_t[:, 0:MT], COPY, scale=-1.0)
+            return noise_t
 
-        out_view = out.rearrange("(b i p) r -> b p i r", i=2, p=P)
+        out_view = out.rearrange("(m p) r -> p m r", p=P)
 
-        def noise_term(pair):
-            y[pair] = work.tile([P, 2, R], F32, name="y", bufs=PAIRS)
-            for i in range(2):
-                m = 2 * pair + i
-                nc.scalar.activation(y[pair][:, i, :], om_rows[:, m, :], COPY, scale=neg_noise[:, m : m + 1])
+        def noise_term(tiles):
+            y[tiles] = keep.tile([P, len(tiles), R], F32, name="y%d" % tiles[0])
+            for i, m in enumerate(tiles):
+                nc.scalar.activation(y[tiles][:, i, :], om_rows[:, m, :], COPY, scale=neg_noise[:, m : m + 1])
 
-        def finish(pair):
-            for part in [slice(0, 2)] if pair < PAIRS - 1 else [slice(0, 1), slice(1, 2)]:
-                nc.vector.tensor_tensor(y[pair][:, part, :], acc[pair][:, part, :], y[pair][:, part, :], ADD)
-                nc.sync.dma_start(out=out_view[pair][:, part, :], in_=y[pair][:, part, :])
+        def finish(tiles):
+            parts = [(0, 1), (1, 2)] if tiles == RESIDENT[0] else [(0, len(tiles))]
+            for i0, i1 in parts:
+                part = y[tiles][:, i0:i1, :]
+                nc.vector.tensor_tensor(part, acc[tiles][:, i0:i1, :], part, ADD)
+                nc.sync.dma_start(out=out_view[:, tiles[0] + i0 : tiles[0] + i1, :], in_=part)
 
-        AHEAD = 2
-        BACK_PER_STEP = 3
-        LATE_EARLY = 3
-        BACK_A = 1
-        BACK_B = 1
-        BACK_C = 1
         to_widen = [(g, k, j) for g in range(NG) for k in range(KG) if SPAN_OF[g, k][0] == g for j in range(PACK)]
         to_project = list(range(UNITS))
         to_back = []
@@ -270,6 +272,11 @@ def tile_weighted_range_power_step_s13_kernel(
                     break
                 widen(*to_widen.pop(0))
 
+        def back_some(count):
+            for item in to_back[:count]:
+                back(*item)
+                to_back.remove(item)
+
         def weigh_step(g):
             step = KG * (g + 1) + AHEAD
             return step + 1 if step <= TENSOR_END else step
@@ -279,13 +286,18 @@ def tile_weighted_range_power_step_s13_kernel(
             interleave_on_tensor(u)
         for s in range(UNITS - KG):
             dst, src = interleave_views(s)
-            cut = BLOCKS // 4 * side[s][-1][0] if s in side else BLOCKS - SHARED_BLOCKS if s >= UNITS - SHARED_UNITS else BLOCKS
+            if s in side:
+                cut = QUARTER * side[s][-1][0]
+            else:
+                cut = BLOCKS - QUARTER if s >= UNITS - SHARED_UNITS else BLOCKS
             nc.scalar.copy(dst[:, :cut], src[:, :cut])
             for q0, q1, bank in side.get(s, ()):
                 nc.scalar.copy(
                     grouped[s][:].rearrange("p (t m j) -> p t m j", t=PACK, j=PACK)[:, :, 32 * q0 : 32 * q1, :],
                     bank[:].rearrange("p (m t) j -> p t m j", t=PACK),
                 )
+            if s == TENSOR_END:
+                nc.scalar.activation(neg_noise[:], noise_t[:, 0:MT], COPY, scale=-1.0)
             ready = [g for g in range(LAST) if weigh_step(g) == s]
             if 1 <= s <= KG:
                 omega_interleave(s - 1)
@@ -301,20 +313,18 @@ def tile_weighted_range_power_step_s13_kernel(
                 omega_quantize(s - 1)
             for g in ready:
                 quantize_v(g)
-                to_back.extend((pair, g) for pair in range(NACC))
+                to_back.extend((tiles, g) for tiles in RESIDENT)
             if s == TENSOR_END - 1:
-                noise_onto_partitions()
+                noise_t = noise_onto_partitions()
             while to_project[0] <= s - AHEAD and to_project[0] // KG <= len(v_grouped):
                 project(to_project.pop(0))
             if s + AHEAD < TENSOR_END:
                 interleave_on_tensor(s + AHEAD)
             if s >= TENSOR_END:
-                for item in to_back[:BACK_PER_STEP]:
-                    back(*item)
-                    to_back.remove(item)
+                back_some(BACK_PER_STEP)
 
         first = UNITS - KG
-        cut = BLOCKS - SHARED_BLOCKS
+        cut = BLOCKS - QUARTER
         views = {}
 
         def scalar_share(u):
@@ -328,9 +338,7 @@ def tile_weighted_range_power_step_s13_kernel(
             new_codes(u)
             quantize_a(u)
             project(u)
-            for item in to_back[:n_back]:
-                back(*item)
-                to_back.remove(item)
+            back_some(n_back)
 
         scalar_share(first)
         quantize_and_project(first - 2, 0)
@@ -344,40 +352,40 @@ def tile_weighted_range_power_step_s13_kernel(
         scalar_share(first + 1)
         vector_share(first + 1)
         quantize_v(LAST - 1)
-        to_back.extend((pair, LAST - 1) for pair in range(NACC))
-        for item in to_back[:BACK_A]:
-            back(*item)
-            to_back.remove(item)
-        quantize_and_project(first, BACK_B)
+        to_back.extend((tiles, LAST - 1) for tiles in RESIDENT)
+        back_some(2)
+        quantize_and_project(first, 1)
         scalar_share(first + 2)
         vector_share(first + 2)
-        quantize_and_project(first + 1, BACK_C)
+        quantize_and_project(first + 1, 1)
 
         u = UNITS - 1
         dst, src = interleave_views(u)
         nc.scalar.copy(dst[:, :, 0:2], src[:, :, 0:2])
         nc.scalar.copy(dst[:, :, 2:3], src[:, :, 2:3])
-        for pair in range(PAIRS):
-            noise_term(pair)
+        for tiles in RESIDENT + LATE:
+            noise_term(tiles)
         nc.vector.tensor_copy(dst[:, :, 3:4], src[:, :, 3:4])
-        quantize_and_project(u - 1, 0)
+        new_codes(u - 1)
+        quantize_a(u - 1)
+        project(u - 1)
         new_codes(u)
         for t0, t1 in ((3, 4), (0, 2), (2, 3)):
             quantize_a(u, t0, t1)
-            project(u, range(t0, t1), closing_t=2)
-        for item in to_back:
-            back(*item)
+            project(u, range(t0, t1), closing_t=2, halves=(0,))
+        project(u, halves=(1,))
+        back_some(NACC)
 
         weigh(LAST)
         for h in range(2):
             quantize_v(LAST, h, h + 1)
-        late = [(pair, g) for pair in range(NACC, PAIRS) for g in range(NG)]
+        late = [(tiles, g) for tiles in LATE for g in range(NG)]
         for item in late[:LATE_EARLY]:
             back(*item)
-        for pair in range(NACC):
-            back(pair, LAST)
-            finish(pair)
-        for pair, g in late[LATE_EARLY:]:
-            back(pair, g)
+        for tiles in RESIDENT:
+            back(tiles, LAST)
+            finish(tiles)
+        for tiles, g in late[LATE_EARLY:]:
+            back(tiles, g)
             if g == LAST:
-                finish(pair)
+                finish(tiles)

@@ -228,17 +228,16 @@ def tile_weighted_range_power_step_s13_kernel(
         def back(tiles, g):
             if g == 0:
                 acc[tiles] = psum.tile([P, len(tiles), R], F32, name="acc%d" % tiles[0], tag=BANK_OF[tiles])
-            for h in range(2):
-                for i, m in enumerate(tiles):
-                    nc.tensor.matmul_mx(
-                        out=acc[tiles][:, i, P * h : P * (h + 1)],
-                        lhsT=b_words[g][:, 2 * P * m : 2 * P * (m + 1)].bitcast(FP4X4),
-                        lhsT_scale=b_scales[:, g, P * m : P * (m + 1)],
-                        rhs=v_codes[g][:, P * h : P * (h + 1)].bitcast(FP8X4),
-                        rhs_scale=v_scales[g][:, P * h : P * (h + 1)],
-                        start=(g == 0 and h == 0 and i == 0),
-                        stop=(g == LAST and h == 1 and i == len(tiles) - 1),
-                    )
+            for i, m in enumerate(tiles):
+                nc.tensor.matmul_mx(
+                    out=acc[tiles][:, i, :],
+                    lhsT=b_words[g][:, 2 * P * m : 2 * P * (m + 1)].bitcast(FP4X4),
+                    lhsT_scale=b_scales[:, g, P * m : P * (m + 1)],
+                    rhs=v_codes[g][:].bitcast(FP8X4),
+                    rhs_scale=v_scales[g][:],
+                    start=(g == 0 and i == 0),
+                    stop=(g == LAST and i == len(tiles) - 1),
+                )
 
         def noise_onto_partitions():
             noise_t = psum.tile([P, P], BF16, name="noise_t", tag="acc%d" % (NACC - 1))

@@ -40,7 +40,13 @@ SPAN_OF = {(g, k): span for k in range(KG) for span in SPANS[k % 2] for g in spa
 TENSOR_END = 14
 THREE_QUARTER_PASS = 2
 SCALAR_WIDENS = 12
-SHARED_UNITS = 5
+SCALAR_UNITS = (0, 1, 2, 3, 4, 5, 6, 7, 11, 12, 14)
+SCALAR_AHEAD = 3
+WIDE_BUFS = 4
+LAST_SHARE = 12
+POOL_GROUPS = (0, 1, 2, 3, 4)
+SHARED_UNITS = 4
+POOL_BLOCKS = 16
 AHEAD = 2
 BACK_PER_STEP = 3 * NACC // (UNITS - KG - TENSOR_END)
 LATE_EARLY = 3
@@ -130,17 +136,20 @@ def tile_weighted_range_power_step_s13_kernel(
         nc.sync.dma_start(out=om_rows[:], in_=omega.rearrange("(m p) r -> p m r", p=P))
 
         planes, side, grouped, a_codes, a_scales = {}, {}, {}, {}, {}
-        om_grouped, z, v_grouped, acc, y = {}, {}, {}, {}, {}
+        om_grouped, z, v_grouped, acc, y, y_half = {}, {}, {}, {}, {}, {}
+
+        def on_scalar(g, k, j):
+            return j == PACK - 1 and g * KG + k in SCALAR_UNITS
 
         def widen(g, k, j):
-            if j == 0:
+            if (g, k) not in planes:
                 width = len(SPAN_OF[g, k])
                 planes[g, k] = work.tile(
-                    [P, PACK, S * width], BF16, name="wide%d" % width, bufs=3 + width, align_bytes=64
+                    [P, PACK, S * width], BF16, name="wide%d" % width, bufs=WIDE_BUFS + width, align_bytes=64
                 )
             in_ = a_raw[g, k][:, j, :].bitcast(FP8)
             scale = a_sc_first[:, 0, j : j + 1] if k == 0 else a_sc_rest[:, k - 1, j : j + 1]
-            if j == PACK - 1 and g * KG + k < SCALAR_WIDENS:
+            if on_scalar(g, k, j):
                 nc.scalar.activation(planes[g, k][:, j, :], in_, COPY, scale=scale)
             else:
                 nc.vector.tensor_scalar(planes[g, k][:, j, :], in_, scale, None, MULT)
@@ -166,10 +175,18 @@ def tile_weighted_range_power_step_s13_kernel(
                     )
 
         def interleave_views(u):
-            grouped[u] = work.tile([P, S * PACK], BF16, name="grouped", bufs=AHEAD + 2, align_bytes=64)
+            if u not in grouped:
+                grouped[u] = work.tile([P, S * PACK], BF16, name="grouped", bufs=AHEAD + 2, align_bytes=64)
             src = unit_planes(u).rearrange("p j (m i t) -> p m t j i", i=2, t=PACK)
             dst = grouped[u][:].rearrange("p (t m i j) -> p m t j i", t=PACK, i=2, j=PACK)
             return dst, src
+
+        def interleave_on_gpsimd(u):
+            interleave_views(u)
+            src = unit_planes(u).rearrange("p j (n t) -> p n t j", t=PACK)
+            dst = grouped[u][:].rearrange("p (t n j) -> p n t j", t=PACK, j=PACK)
+            nc.gpsimd.tensor_scalar(dst[:, : 2 * POOL_BLOCKS], src[:, : 2 * POOL_BLOCKS], 1.0, 0.0, MULT, ADD)
+            pooled.add(u)
 
         def new_codes(u):
             a_codes[u] = work.tile([P, S], U32, name="codes", bufs=6, align_bytes=64)
@@ -247,7 +264,12 @@ def tile_weighted_range_power_step_s13_kernel(
         out_view = out.rearrange("(m p) r -> p m r", p=P)
 
         def noise_term(tiles):
-            y[tiles] = keep.tile([P, len(tiles), R], F32, name="y%d" % tiles[0])
+            half = tiles[0] // (MT // 2)
+            if half not in y_half:
+                y_half[half] = work.tile(
+                    [P, MT // 2, R], F32, name="y%d" % half, tag="wide2", bufs=WIDE_BUFS + 2, align_bytes=64
+                )
+            y[tiles] = y_half[half][:, tiles[0] % (MT // 2) : tiles[0] % (MT // 2) + len(tiles), :]
             for i, m in enumerate(tiles):
                 nc.scalar.activation(y[tiles][:, i, :], om_rows[:, m, :], COPY, scale=neg_noise[:, m : m + 1])
 
@@ -262,6 +284,7 @@ def tile_weighted_range_power_step_s13_kernel(
         to_project = list(range(UNITS))
         to_back = []
         banks = []
+        pooled = set()
 
         def widen_for(u):
             while to_widen:
@@ -270,6 +293,11 @@ def tile_weighted_range_power_step_s13_kernel(
                 if opens > u + 1 or (opens == u + 1 and (len(SPAN_OF[g, k]) == 1 or j >= PACK // 2)):
                     break
                 widen(*to_widen.pop(0))
+
+        def scalar_widen_for(u):
+            for item in [x for x in to_widen if on_scalar(*x) and x[0] * KG + x[1] <= u]:
+                to_widen.remove(item)
+                widen(*item)
 
         def back_some(count):
             for item in to_back[:count]:
@@ -289,7 +317,9 @@ def tile_weighted_range_power_step_s13_kernel(
                 cut = QUARTER * side[s][-1][0]
             else:
                 cut = BLOCKS - QUARTER if s >= UNITS - SHARED_UNITS else BLOCKS
-            nc.scalar.copy(dst[:, :cut], src[:, :cut])
+            lo = POOL_BLOCKS if s in pooled else 0
+            if cut > lo:
+                nc.scalar.copy(dst[:, lo:cut], src[:, lo:cut])
             for q0, q1, bank in side.get(s, ()):
                 nc.scalar.copy(
                     grouped[s][:].rearrange("p (t m j) -> p t m j", t=PACK, j=PACK)[:, :, 32 * q0 : 32 * q1, :],
@@ -300,38 +330,52 @@ def tile_weighted_range_power_step_s13_kernel(
             ready = [g for g in range(LAST) if weigh_step(g) == s]
             if 1 <= s <= KG:
                 omega_interleave(s - 1)
+            scalar_widen_for(s + SCALAR_AHEAD)
+            pool = [g for g in ready if g in POOL_GROUPS]
+            opens = SPAN_OF[divmod(s + AHEAD, KG)][0] == (s + AHEAD) // KG
+            if pool and not opens:
+                widen_for(s + AHEAD)
             if s >= AHEAD:
                 new_codes(s - AHEAD)
                 quantize_a(s - AHEAD)
+            for g in range(LAST):
+                if weigh_step(g) == s - 1:
+                    quantize_v(g)
+                    to_back.extend((tiles, g) for tiles in RESIDENT)
+            if pool:
+                widen_for(s + AHEAD)
             for g in ready:
                 weigh(g)
+            if pool:
+                interleave_on_gpsimd(s + AHEAD)
             widen_for(s + AHEAD)
             if s not in side and cut < BLOCKS:
                 nc.vector.tensor_copy(dst[:, cut:], src[:, cut:])
             if 1 <= s <= KG:
                 omega_quantize(s - 1)
-            for g in ready:
-                quantize_v(g)
-                to_back.extend((tiles, g) for tiles in RESIDENT)
             if s == TENSOR_END - 1:
                 noise_t = noise_onto_partitions()
+            if s >= TENSOR_END and ready:
+                back_some(BACK_PER_STEP)
             while to_project[0] <= s - AHEAD and to_project[0] // KG <= len(v_grouped):
                 project(to_project.pop(0))
             if s + AHEAD < TENSOR_END:
                 interleave_on_tensor(s + AHEAD)
-            if s >= TENSOR_END:
+            if s >= TENSOR_END and not ready:
                 back_some(BACK_PER_STEP)
 
         first = UNITS - KG
-        cut = BLOCKS - QUARTER
+        cut = BLOCKS - LAST_SHARE
         views = {}
 
         def scalar_share(u):
             views[u] = interleave_views(u)
-            nc.scalar.copy(views[u][0][:, :cut], views[u][1][:, :cut])
+            lo = POOL_BLOCKS if u in pooled else 0
+            nc.scalar.copy(views[u][0][:, lo:cut], views[u][1][:, lo:cut])
 
         def vector_share(u):
-            nc.vector.tensor_copy(views[u][0][:, cut:], views[u][1][:, cut:])
+            if cut < BLOCKS:
+                nc.vector.tensor_copy(views[u][0][:, cut:], views[u][1][:, cut:])
 
         def quantize_and_project(u, n_back):
             new_codes(u)
@@ -344,10 +388,12 @@ def tile_weighted_range_power_step_s13_kernel(
         for item in to_widen[:2]:
             widen(*item)
         quantize_and_project(first - 1, NACC)
+        vector_share(first)
         for item in to_widen[2:]:
             widen(*item)
-        vector_share(first)
         weigh(LAST - 1)
+        if LAST - 1 in POOL_GROUPS:
+            interleave_on_gpsimd(first + 2)
         scalar_share(first + 1)
         vector_share(first + 1)
         quantize_v(LAST - 1)
@@ -367,11 +413,12 @@ def tile_weighted_range_power_step_s13_kernel(
         nc.vector.tensor_copy(dst[:, :, 3:4], src[:, :, 3:4])
         new_codes(u - 1)
         quantize_a(u - 1)
-        project(u - 1)
+        project(u - 1, halves=(0,))
         new_codes(u)
         for t0, t1 in ((3, 4), (0, 2), (2, 3)):
             quantize_a(u, t0, t1)
             project(u, range(t0, t1), closing_t=2, halves=(0,))
+        project(u - 1, halves=(1,))
         project(u, halves=(1,))
         back_some(NACC)
 

@@ -37,18 +37,24 @@ BANK_OF = dict([(tiles, "acc%d" % b) for b, tiles in enumerate(RESIDENT)] + list
 SPANS = (((0,), (1, 2), (3, 4), (5,)), ((0,), (1,), (2, 3), (4, 5)))
 SPAN_OF = {(g, k): span for k in range(KG) for span in SPANS[k % 2] for g in span}
 
+UNIT = [(g, k) for g in range(LAST) for k in range(KG)] + [(LAST, k) for k in (1, 3, 0, 2)]
+POS = {gk: u for u, gk in enumerate(UNIT)}
+
 TENSOR_END = 14
 THREE_QUARTER_PASS = 2
 SCALAR_WIDENS = 12
 SCALAR_UNITS = (0, 1, 2, 3, 4, 5, 6, 7, 11, 12, 14)
 SCALAR_AHEAD = 3
 WIDE_BUFS = 4
-LAST_SHARE = 12
+LAST_SHARE = 4
+BACK_LAST = 1
+BACK_FIRST = 3
+EARLY_PLANES = 3
 POOL_GROUPS = (0, 1, 2, 3, 4)
 SHARED_UNITS = 4
-POOL_BLOCKS = 16
+POOL_BLOCKS = 24
 AHEAD = 2
-BACK_PER_STEP = 3 * NACC // (UNITS - KG - TENSOR_END)
+BACK_PER_STEP = 4
 LATE_EARLY = 3
 
 
@@ -139,7 +145,7 @@ def tile_weighted_range_power_step_s13_kernel(
         om_grouped, z, v_grouped, acc, y, y_half = {}, {}, {}, {}, {}, {}
 
         def on_scalar(g, k, j):
-            return j == PACK - 1 and g * KG + k in SCALAR_UNITS
+            return j == PACK - 1 and POS[g, k] in SCALAR_UNITS
 
         def widen(g, k, j):
             if (g, k) not in planes:
@@ -155,7 +161,7 @@ def tile_weighted_range_power_step_s13_kernel(
                 nc.vector.tensor_scalar(planes[g, k][:, j, :], in_, scale, None, MULT)
 
         def unit_planes(u):
-            g, k = divmod(u, KG)
+            g, k = UNIT[u]
             first = SPAN_OF[g, k][0]
             return planes[first, k][:, :, S * (g - first) : S * (g - first + 1)]
 
@@ -209,9 +215,9 @@ def tile_weighted_range_power_step_s13_kernel(
             nc.vector.quantize_mx(om_codes[k][:].bitcast(FP8X4), om_scales[k][:], om_grouped[k][:])
 
         def project(u, ts=range(PACK), closing_t=PACK - 1, halves=range(2)):
-            g, k = divmod(u, KG)
+            g, k = UNIT[u]
             for h in halves:
-                if k == 0:
+                if u % KG == 0:
                     z[g, h] = psum.tile([P, PACK, P], F32, name="z%d_%d" % (g, h), tag="z%d" % h)
                 for t in ts:
                     nc.tensor.matmul_mx(
@@ -220,8 +226,8 @@ def tile_weighted_range_power_step_s13_kernel(
                         lhsT_scale=a_scales[u][:, P * t : P * (t + 1)],
                         rhs=om_codes[k][:, P * h : P * (h + 1)].bitcast(FP8X4),
                         rhs_scale=om_scales[k][:, P * h : P * (h + 1)],
-                        start=(k == 0 and t == 0),
-                        stop=(k == KG - 1 and t == closing_t),
+                        start=(u % KG == 0 and t == 0),
+                        stop=(u % KG == KG - 1 and t == closing_t),
                     )
 
         def weigh(g):
@@ -245,15 +251,17 @@ def tile_weighted_range_power_step_s13_kernel(
         def back(tiles, g):
             if g == 0:
                 acc[tiles] = psum.tile([P, len(tiles), R], F32, name="acc%d" % tiles[0], tag=BANK_OF[tiles])
-            for i, m in enumerate(tiles):
+            width = P if (tiles, g) == (RESIDENT[0], LAST) else R
+            passes = [(c, i, m) for c in range(0, R, width) for i, m in enumerate(tiles)]
+            for c, i, m in passes:
                 nc.tensor.matmul_mx(
-                    out=acc[tiles][:, i, :],
+                    out=acc[tiles][:, i, c : c + width],
                     lhsT=b_words[g][:, 2 * P * m : 2 * P * (m + 1)].bitcast(FP4X4),
                     lhsT_scale=b_scales[:, g, P * m : P * (m + 1)],
-                    rhs=v_codes[g][:].bitcast(FP8X4),
-                    rhs_scale=v_scales[g][:],
-                    start=(g == 0 and i == 0),
-                    stop=(g == LAST and i == len(tiles) - 1),
+                    rhs=v_codes[g][:, c : c + width].bitcast(FP8X4),
+                    rhs_scale=v_scales[g][:, c : c + width],
+                    start=(g == 0 and (c, i, m) == passes[0]),
+                    stop=(g == LAST and (c, i, m) == passes[-1]),
                 )
 
         def noise_onto_partitions():
@@ -280,7 +288,7 @@ def tile_weighted_range_power_step_s13_kernel(
                 nc.vector.tensor_tensor(part, acc[tiles][:, i0:i1, :], part, ADD)
                 nc.sync.dma_start(out=out_view[:, tiles[0] + i0 : tiles[0] + i1, :], in_=part)
 
-        to_widen = [(g, k, j) for g in range(NG) for k in range(KG) if SPAN_OF[g, k][0] == g for j in range(PACK)]
+        to_widen = [(g, k, j) for g, k in UNIT if SPAN_OF[g, k][0] == g for j in range(PACK)]
         to_project = list(range(UNITS))
         to_back = []
         banks = []
@@ -289,13 +297,22 @@ def tile_weighted_range_power_step_s13_kernel(
         def widen_for(u):
             while to_widen:
                 g, k, j = to_widen[0]
-                opens = g * KG + k
+                opens = POS[g, k]
                 if opens > u + 1 or (opens == u + 1 and (len(SPAN_OF[g, k]) == 1 or j >= PACK // 2)):
                     break
                 widen(*to_widen.pop(0))
 
+        def widen_unit(u):
+            while to_widen and POS[to_widen[0][:2]] <= u:
+                widen(*to_widen.pop(0))
+
+        def widen_next():
+            item = [x for x in to_widen if not on_scalar(*x)][0]
+            to_widen.remove(item)
+            widen(*item)
+
         def scalar_widen_for(u):
-            for item in [x for x in to_widen if on_scalar(*x) and x[0] * KG + x[1] <= u]:
+            for item in [x for x in to_widen if on_scalar(*x) and POS[x[:2]] <= u]:
                 to_widen.remove(item)
                 widen(*item)
 
@@ -332,9 +349,6 @@ def tile_weighted_range_power_step_s13_kernel(
                 omega_interleave(s - 1)
             scalar_widen_for(s + SCALAR_AHEAD)
             pool = [g for g in ready if g in POOL_GROUPS]
-            opens = SPAN_OF[divmod(s + AHEAD, KG)][0] == (s + AHEAD) // KG
-            if pool and not opens:
-                widen_for(s + AHEAD)
             if s >= AHEAD:
                 new_codes(s - AHEAD)
                 quantize_a(s - AHEAD)
@@ -343,7 +357,9 @@ def tile_weighted_range_power_step_s13_kernel(
                     quantize_v(g)
                     to_back.extend((tiles, g) for tiles in RESIDENT)
             if pool:
-                widen_for(s + AHEAD)
+                widen_for(s + AHEAD - 1)
+                widen_unit(s + AHEAD)
+                widen_next()
             for g in ready:
                 weigh(g)
             if pool:
@@ -357,9 +373,15 @@ def tile_weighted_range_power_step_s13_kernel(
                 noise_t = noise_onto_partitions()
             if s >= TENSOR_END and ready:
                 back_some(BACK_PER_STEP)
-            while to_project[0] <= s - AHEAD and to_project[0] // KG <= len(v_grouped):
-                project(to_project.pop(0))
-            if s + AHEAD < TENSOR_END:
+            if s + AHEAD < TENSOR_END and ready:
+                interleave_on_tensor(s + AHEAD)
+            due = [u for u in to_project if u <= s - AHEAD and u // KG <= len(v_grouped)]
+            for h in range(2):
+                for u in due:
+                    project(u, halves=(h,))
+            for u in due:
+                to_project.remove(u)
+            if s + AHEAD < TENSOR_END and not ready:
                 interleave_on_tensor(s + AHEAD)
             if s >= TENSOR_END and not ready:
                 back_some(BACK_PER_STEP)
@@ -385,24 +407,26 @@ def tile_weighted_range_power_step_s13_kernel(
 
         scalar_share(first)
         quantize_and_project(first - 2, 0)
-        for item in to_widen[:2]:
+        widen_next()
+        for item in [x for x in to_widen if POS[x[:2]] == UNITS - 1 and not on_scalar(*x)][:EARLY_PLANES]:
+            to_widen.remove(item)
             widen(*item)
         quantize_and_project(first - 1, NACC)
+        widen_unit(first + 2)
         vector_share(first)
-        for item in to_widen[2:]:
-            widen(*item)
         weigh(LAST - 1)
-        if LAST - 1 in POOL_GROUPS:
-            interleave_on_gpsimd(first + 2)
         scalar_share(first + 1)
-        vector_share(first + 1)
+        interleave_on_gpsimd(first + 2)
+        scalar_widen_for(UNITS - 1)
+        quantize_and_project(first, 0)
         quantize_v(LAST - 1)
         to_back.extend((tiles, LAST - 1) for tiles in RESIDENT)
-        back_some(2)
-        quantize_and_project(first, 1)
+        back_some(BACK_FIRST)
+        widen_unit(UNITS - 1)
+        vector_share(first + 1)
+        quantize_and_project(first + 1, BACK_LAST)
         scalar_share(first + 2)
         vector_share(first + 2)
-        quantize_and_project(first + 1, 1)
 
         u = UNITS - 1
         dst, src = interleave_views(u)

@@ -40,22 +40,32 @@ SPAN_OF = {(g, k): span for k in range(KG) for span in SPANS[k % 2] for g in spa
 UNIT = [(g, k) for g in range(LAST) for k in range(KG)] + [(LAST, k) for k in (1, 3, 0, 2)]
 POS = {gk: u for u, gk in enumerate(UNIT)}
 
-TENSOR_END = 14
-THREE_QUARTER_PASS = 2
-SCALAR_WIDENS = 12
-SCALAR_UNITS = (0, 1, 2, 3, 4, 5, 6, 7, 11, 12, 14)
-SCALAR_AHEAD = 3
-WIDE_BUFS = 4
-LAST_SHARE = 4
-BACK_LAST = 1
-BACK_FIRST = 3
-EARLY_PLANES = 3
-POOL_GROUPS = (0, 1, 2, 3, 4)
-SHARED_UNITS = 4
-POOL_BLOCKS = 24
 AHEAD = 2
-BACK_PER_STEP = 4
-LATE_EARLY = 3
+TENSOR_END = 15
+THREE_QUARTER_END = 7
+BACK_START = TENSOR_END - 1
+BACK_PER_STEP = 3 * NACC // (UNITS - KG - BACK_START)
+POOL_BLOCKS = 24
+EARLY_PLANES = 2
+LATE_EARLY = 2
+WIDE_BUFS = {1: 5, 2: 6}
+
+
+def weigh_step(g):
+    step = KG * (g + 1) + AHEAD
+    return step + 1 if step <= BACK_START else step
+
+
+POOL_UNITS = [weigh_step(g) + AHEAD for g in range(LAST - 1)] + [UNITS - 2]
+
+
+def on_scalar(g, k, j):
+    u = POS[g, k]
+    if u < AHEAD:
+        return j == 1
+    if u < KG:
+        return j >= PACK - 2
+    return j == PACK - 1 and u < TENSOR_END and u not in POOL_UNITS
 
 
 def tile_weighted_range_power_step_s13_kernel(
@@ -144,14 +154,11 @@ def tile_weighted_range_power_step_s13_kernel(
         planes, side, grouped, a_codes, a_scales = {}, {}, {}, {}, {}
         om_grouped, z, v_grouped, acc, y, y_half = {}, {}, {}, {}, {}, {}
 
-        def on_scalar(g, k, j):
-            return j == PACK - 1 and POS[g, k] in SCALAR_UNITS
-
         def widen(g, k, j):
             if (g, k) not in planes:
                 width = len(SPAN_OF[g, k])
                 planes[g, k] = work.tile(
-                    [P, PACK, S * width], BF16, name="wide%d" % width, bufs=WIDE_BUFS + width, align_bytes=64
+                    [P, PACK, S * width], BF16, name="wide%d" % width, bufs=WIDE_BUFS[width], align_bytes=64
                 )
             in_ = a_raw[g, k][:, j, :].bitcast(FP8)
             scale = a_sc_first[:, 0, j : j + 1] if k == 0 else a_sc_rest[:, k - 1, j : j + 1]
@@ -165,11 +172,15 @@ def tile_weighted_range_power_step_s13_kernel(
             first = SPAN_OF[g, k][0]
             return planes[first, k][:, :, S * (g - first) : S * (g - first + 1)]
 
+        def borrow_bank(step):
+            b = lent_until.index(min(lent_until))
+            lent_until[b] = step
+            return "acc%d" % b
+
         def interleave_on_tensor(u):
             side[u] = []
-            for q0, q1 in ((2, 4), (1, 2)) if u % KG == THREE_QUARTER_PASS else ((2, 4),):
-                bank = psum.tile([P, P * (q1 - q0), PACK], BF16, name="side", tag="acc%d" % (len(banks) % NACC))
-                banks.append(bank)
+            for q0, q1 in ((2, 4), (1, 2)) if AHEAD <= u < THREE_QUARTER_END else ((2, 4),):
+                bank = psum.tile([P, P * (q1 - q0), PACK], BF16, name="side", tag=borrow_bank(u))
                 side[u].append((q0, q1, bank))
                 for q in range(q0, q1):
                     nc.tensor.matmul(
@@ -192,7 +203,6 @@ def tile_weighted_range_power_step_s13_kernel(
             src = unit_planes(u).rearrange("p j (n t) -> p n t j", t=PACK)
             dst = grouped[u][:].rearrange("p (t n j) -> p n t j", t=PACK, j=PACK)
             nc.gpsimd.tensor_scalar(dst[:, : 2 * POOL_BLOCKS], src[:, : 2 * POOL_BLOCKS], 1.0, 0.0, MULT, ADD)
-            pooled.add(u)
 
         def new_codes(u):
             a_codes[u] = work.tile([P, S], U32, name="codes", bufs=6, align_bytes=64)
@@ -265,7 +275,7 @@ def tile_weighted_range_power_step_s13_kernel(
                 )
 
         def noise_onto_partitions():
-            noise_t = psum.tile([P, P], BF16, name="noise_t", tag="acc%d" % (NACC - 1))
+            noise_t = psum.tile([P, P], BF16, name="noise_t", tag=borrow_bank(BACK_START))
             nc.tensor.transpose(noise_t[:], noise_rows[:], ident[:])
             return noise_t
 
@@ -275,7 +285,7 @@ def tile_weighted_range_power_step_s13_kernel(
             half = tiles[0] // (MT // 2)
             if half not in y_half:
                 y_half[half] = work.tile(
-                    [P, MT // 2, R], F32, name="y%d" % half, tag="wide2", bufs=WIDE_BUFS + 2, align_bytes=64
+                    [P, MT // 2, R], F32, name="y%d" % half, tag="wide2", bufs=WIDE_BUFS[2], align_bytes=64
                 )
             y[tiles] = y_half[half][:, tiles[0] % (MT // 2) : tiles[0] % (MT // 2) + len(tiles), :]
             for i, m in enumerate(tiles):
@@ -291,8 +301,7 @@ def tile_weighted_range_power_step_s13_kernel(
         to_widen = [(g, k, j) for g, k in UNIT if SPAN_OF[g, k][0] == g for j in range(PACK)]
         to_project = list(range(UNITS))
         to_back = []
-        banks = []
-        pooled = set()
+        lent_until = [b - NACC for b in range(NACC)]
 
         def widen_for(u):
             while to_widen:
@@ -316,39 +325,39 @@ def tile_weighted_range_power_step_s13_kernel(
                 to_widen.remove(item)
                 widen(*item)
 
-        def back_some(count):
-            for item in to_back[:count]:
+        def back_some(count, s=UNITS):
+            for item in [x for x in to_back if lent_until[RESIDENT.index(x[0])] <= s][:count]:
                 back(*item)
                 to_back.remove(item)
 
-        def weigh_step(g):
-            step = KG * (g + 1) + AHEAD
-            return step + 1 if step <= TENSOR_END else step
+        def scalar_share(u):
+            dst, src = interleave_views(u)
+            lo = POOL_BLOCKS if u in POOL_UNITS else 0
+            hi = QUARTER * side[u][-1][0] if u in side else BLOCKS
+            nc.scalar.copy(dst[:, lo:hi], src[:, lo:hi])
+
+        def tensor_other(s):
+            if s + AHEAD < TENSOR_END:
+                interleave_on_tensor(s + AHEAD)
+            if s >= BACK_START:
+                back_some(BACK_PER_STEP, s)
 
         widen_for(AHEAD - 1)
         for u in range(AHEAD):
             interleave_on_tensor(u)
         for s in range(UNITS - KG):
-            dst, src = interleave_views(s)
-            if s in side:
-                cut = QUARTER * side[s][-1][0]
-            else:
-                cut = BLOCKS - QUARTER if s >= UNITS - SHARED_UNITS else BLOCKS
-            lo = POOL_BLOCKS if s in pooled else 0
-            if cut > lo:
-                nc.scalar.copy(dst[:, lo:cut], src[:, lo:cut])
+            scalar_share(s)
+            scalar_widen_for(s + AHEAD + 1)
             for q0, q1, bank in side.get(s, ()):
                 nc.scalar.copy(
                     grouped[s][:].rearrange("p (t m j) -> p t m j", t=PACK, j=PACK)[:, :, 32 * q0 : 32 * q1, :],
                     bank[:].rearrange("p (m t) j -> p t m j", t=PACK),
                 )
-            if s == TENSOR_END:
+            if s == BACK_START:
                 nc.scalar.activation(neg_noise[:], noise_t[:, 0:MT], COPY, scale=-1.0)
             ready = [g for g in range(LAST) if weigh_step(g) == s]
             if 1 <= s <= KG:
                 omega_interleave(s - 1)
-            scalar_widen_for(s + SCALAR_AHEAD)
-            pool = [g for g in ready if g in POOL_GROUPS]
             if s >= AHEAD:
                 new_codes(s - AHEAD)
                 quantize_a(s - AHEAD)
@@ -356,48 +365,28 @@ def tile_weighted_range_power_step_s13_kernel(
                 if weigh_step(g) == s - 1:
                     quantize_v(g)
                     to_back.extend((tiles, g) for tiles in RESIDENT)
-            if pool:
-                widen_for(s + AHEAD - 1)
+            for g in ready:
                 widen_unit(s + AHEAD)
                 widen_next()
-            for g in ready:
                 weigh(g)
-            if pool:
                 interleave_on_gpsimd(s + AHEAD)
             widen_for(s + AHEAD)
-            if s not in side and cut < BLOCKS:
-                nc.vector.tensor_copy(dst[:, cut:], src[:, cut:])
             if 1 <= s <= KG:
                 omega_quantize(s - 1)
-            if s == TENSOR_END - 1:
+            if s == BACK_START - 1:
                 noise_t = noise_onto_partitions()
-            if s >= TENSOR_END and ready:
-                back_some(BACK_PER_STEP)
-            if s + AHEAD < TENSOR_END and ready:
-                interleave_on_tensor(s + AHEAD)
+            if ready:
+                tensor_other(s)
             due = [u for u in to_project if u <= s - AHEAD and u // KG <= len(v_grouped)]
             for h in range(2):
                 for u in due:
                     project(u, halves=(h,))
             for u in due:
                 to_project.remove(u)
-            if s + AHEAD < TENSOR_END and not ready:
-                interleave_on_tensor(s + AHEAD)
-            if s >= TENSOR_END and not ready:
-                back_some(BACK_PER_STEP)
+            if not ready:
+                tensor_other(s)
 
         first = UNITS - KG
-        cut = BLOCKS - LAST_SHARE
-        views = {}
-
-        def scalar_share(u):
-            views[u] = interleave_views(u)
-            lo = POOL_BLOCKS if u in pooled else 0
-            nc.scalar.copy(views[u][0][:, lo:cut], views[u][1][:, lo:cut])
-
-        def vector_share(u):
-            if cut < BLOCKS:
-                nc.vector.tensor_copy(views[u][0][:, cut:], views[u][1][:, cut:])
 
         def quantize_and_project(u, n_back):
             new_codes(u)
@@ -408,25 +397,21 @@ def tile_weighted_range_power_step_s13_kernel(
         scalar_share(first)
         quantize_and_project(first - 2, 0)
         widen_next()
-        for item in [x for x in to_widen if POS[x[:2]] == UNITS - 1 and not on_scalar(*x)][:EARLY_PLANES]:
+        for item in [x for x in to_widen if POS[x[:2]] == UNITS - 1][:EARLY_PLANES]:
             to_widen.remove(item)
             widen(*item)
-        quantize_and_project(first - 1, NACC)
+        quantize_and_project(first - 1, 2 * NACC)
         widen_unit(first + 2)
-        vector_share(first)
         weigh(LAST - 1)
         scalar_share(first + 1)
         interleave_on_gpsimd(first + 2)
-        scalar_widen_for(UNITS - 1)
         quantize_and_project(first, 0)
+        widen_unit(UNITS - 1)
+        scalar_share(first + 2)
         quantize_v(LAST - 1)
         to_back.extend((tiles, LAST - 1) for tiles in RESIDENT)
-        back_some(BACK_FIRST)
-        widen_unit(UNITS - 1)
-        vector_share(first + 1)
-        quantize_and_project(first + 1, BACK_LAST)
-        scalar_share(first + 2)
-        vector_share(first + 2)
+        back_some(NACC // 2)
+        quantize_and_project(first + 1, 0)
 
         u = UNITS - 1
         dst, src = interleave_views(u)

@@ -180,11 +180,11 @@ def tile_weighted_range_power_step_s13_kernel(
         def interleave_on_tensor(u):
             side[u] = []
             for q0, q1 in ((2, 4), (1, 2)) if AHEAD <= u < THREE_QUARTER_END else ((2, 4),):
-                bank = psum.tile([P, P * (q1 - q0), PACK], BF16, name="side", tag=borrow_bank(u))
+                bank = psum.tile([P, PACK, 32 * (q1 - q0), PACK], BF16, name="side", tag=borrow_bank(u))
                 side[u].append((q0, q1, bank))
                 for q in range(q0, q1):
                     nc.tensor.matmul(
-                        bank[:, P * (q - q0) : P * (q - q0 + 1), :].rearrange("p n j -> p j n"),
+                        bank[:, :, 32 * (q - q0) : 32 * (q - q0 + 1), :].rearrange("p t m j -> p j m t"),
                         lhsT=ident[:],
                         rhs=unit_planes(u)[:, :, P * q : P * (q + 1)],
                         start=True,
@@ -351,7 +351,7 @@ def tile_weighted_range_power_step_s13_kernel(
             for q0, q1, bank in side.get(s, ()):
                 nc.scalar.copy(
                     grouped[s][:].rearrange("p (t m j) -> p t m j", t=PACK, j=PACK)[:, :, 32 * q0 : 32 * q1, :],
-                    bank[:].rearrange("p (m t) j -> p t m j", t=PACK),
+                    bank[:],
                 )
             if s == BACK_START:
                 nc.scalar.activation(neg_noise[:], noise_t[:, 0:MT], COPY, scale=-1.0)

@@ -63,7 +63,7 @@ def on_scalar(g, k, j):
     u = POS[g, k]
     if u < AHEAD:
         return j == 1
-    if u < KG:
+    if u == KG - 1:
         return j >= PACK - 2
     return j == PACK - 1 and u < TENSOR_END and u not in POOL_UNITS
 
@@ -128,23 +128,26 @@ def tile_weighted_range_power_step_s13_kernel(
         load_a(0, 2)
         load_om(0)
         load_a(0, 3)
-        for k in range(KG - 1):
-            load_a(1, k)
-            load_om(k + 1)
+        load_om(1)
+        load_a(1, 0)
+        load_a(1, 1)
+        load_om(2)
+        load_a(1, 2)
+        load_om(3)
         load_a(1, 3)
         nc.sync.dma_start(out=w_sb[:], in_=sample_w.rearrange("(g p j) -> p g j", p=P, j=PACK))
-        nc.sync.dma_start(out=noise_rows[0:MT, :], in_=noise_var.rearrange("(m p) -> m p", p=P))
         load_a(2, 1)
         load_a(2, 3)
+        load_a(3, 0)
+        load_a(3, 2)
+        load_a(4, 1)
+        nc.sync.dma_start(out=noise_rows[0:MT, :], in_=noise_var.rearrange("(m p) -> m p", p=P))
         for q in range(4):
             nc.sync.dma_start(out=b_scales[q:P:32].bitcast(I32), in_=b_sc_view[q:16:4])
         load_b(0)
-        load_a(3, 0)
-        load_a(3, 2)
         load_b(1)
-        load_a(4, 1)
-        load_b(2)
         load_a(4, 3)
+        load_b(2)
         load_a(5, 0)
         load_a(5, 2)
         for g in range(3, NG):
@@ -307,7 +310,7 @@ def tile_weighted_range_power_step_s13_kernel(
             while to_widen:
                 g, k, j = to_widen[0]
                 opens = POS[g, k]
-                if opens > u + 1 or (opens == u + 1 and (len(SPAN_OF[g, k]) == 1 or j >= PACK // 2)):
+                if opens > u + 1 or (opens == u + 1 and (len(SPAN_OF[g, k]) == 1 or j >= PACK // 2 or opens == KG)):
                     break
                 widen(*to_widen.pop(0))
 
@@ -347,7 +350,7 @@ def tile_weighted_range_power_step_s13_kernel(
             interleave_on_tensor(u)
         for s in range(UNITS - KG):
             scalar_share(s)
-            scalar_widen_for(s + AHEAD + 1)
+            scalar_widen_for(s + AHEAD + min(s, 1))
             for q0, q1, bank in side.get(s, ()):
                 nc.scalar.copy(
                     grouped[s][:].rearrange("p (t m j) -> p t m j", t=PACK, j=PACK)[:, :, 32 * q0 : 32 * q1, :],

@@ -247,9 +247,9 @@ def tile_weighted_range_power_step_s13_kernel(
             v_grouped[g] = work.tile([P, 2, P * PACK], BF16, name="v_grouped", bufs=2, align_bytes=64)
             for h in range(2):
                 nc.vector.tensor_tensor(
-                    v_grouped[g][:, h, :].rearrange("p (c i t) -> p c t i", i=2, t=PACK),
-                    z[g, h][:].rearrange("p t (c i) -> p c t i", i=2),
-                    w_sb[:, g : g + 1, :].unsqueeze(3).to_broadcast([P, P // 2, PACK, 2]),
+                    v_grouped[g][:, h, :].rearrange("p (c t) -> p c t", t=PACK),
+                    z[g, h][:].rearrange("p t c -> p c t"),
+                    w_sb[:, g : g + 1, :].to_broadcast([P, P, PACK]),
                     MULT,
                 )
 

@@ -44,10 +44,9 @@ AHEAD = 2
 TENSOR_END = 15
 THREE_QUARTER_END = 7
 BACK_START = TENSOR_END - 1
-BACK_PER_STEP = 3 * NACC // (UNITS - KG - BACK_START)
+BACK_PER_STEP = 4
 POOL_BLOCKS = 24
-EARLY_PLANES = 2
-LATE_EARLY = 2
+LATE_EARLY = 3
 WIDE_BUFS = {1: 5, 2: 6}
 
 
@@ -56,7 +55,7 @@ def weigh_step(g):
     return step + 1 if step <= BACK_START else step
 
 
-POOL_UNITS = [weigh_step(g) + AHEAD for g in range(LAST - 1)] + [UNITS - 2]
+POOL_UNITS = [weigh_step(g) + AHEAD for g in range(LAST - 2)] + [KG * LAST - 1, UNITS - 2]
 
 
 def on_scalar(g, k, j):
@@ -310,6 +309,8 @@ def tile_weighted_range_power_step_s13_kernel(
             while to_widen:
                 g, k, j = to_widen[0]
                 opens = POS[g, k]
+                if opens == u == POOL_UNITS[LAST - 2] and j == PACK - 1:
+                    break
                 if opens > u + 1 or (opens == u + 1 and (len(SPAN_OF[g, k]) == 1 or j >= PACK // 2 or opens == KG)):
                     break
                 widen(*to_widen.pop(0))
@@ -367,12 +368,13 @@ def tile_weighted_range_power_step_s13_kernel(
             for g in range(LAST):
                 if weigh_step(g) == s - 1:
                     quantize_v(g)
-                    to_back.extend((tiles, g) for tiles in RESIDENT)
+                    if g < LAST - 2:
+                        to_back.extend((tiles, g) for tiles in RESIDENT)
             for g in ready:
                 widen_unit(s + AHEAD)
                 widen_next()
                 weigh(g)
-                interleave_on_gpsimd(s + AHEAD)
+                interleave_on_gpsimd(POOL_UNITS[g])
             widen_for(s + AHEAD)
             if 1 <= s <= KG:
                 omega_quantize(s - 1)
@@ -391,30 +393,29 @@ def tile_weighted_range_power_step_s13_kernel(
 
         first = UNITS - KG
 
-        def quantize_and_project(u, n_back):
+        def quantize_and_project(u):
             new_codes(u)
             quantize_a(u)
             project(u)
-            back_some(n_back)
 
         scalar_share(first)
-        quantize_and_project(first - 2, 0)
+        quantize_and_project(first - 2)
         widen_next()
-        for item in [x for x in to_widen if POS[x[:2]] == UNITS - 1][:EARLY_PLANES]:
-            to_widen.remove(item)
-            widen(*item)
-        quantize_and_project(first - 1, 2 * NACC)
+        quantize_and_project(first - 1)
+        to_back.extend((tiles, LAST - 2) for tiles in RESIDENT)
+        back_some(len(to_back))
         widen_unit(first + 2)
+        widen_next()
         weigh(LAST - 1)
         scalar_share(first + 1)
-        interleave_on_gpsimd(first + 2)
-        quantize_and_project(first, 0)
-        widen_unit(UNITS - 1)
+        interleave_on_gpsimd(POOL_UNITS[LAST - 1])
+        quantize_and_project(first)
         scalar_share(first + 2)
         quantize_v(LAST - 1)
+        widen_unit(UNITS - 1)
         to_back.extend((tiles, LAST - 1) for tiles in RESIDENT)
-        back_some(NACC // 2)
-        quantize_and_project(first + 1, 0)
+        back_some(NACC - 1)
+        quantize_and_project(first + 1)
 
         u = UNITS - 1
         dst, src = interleave_views(u)
@@ -432,7 +433,7 @@ def tile_weighted_range_power_step_s13_kernel(
             project(u, range(t0, t1), closing_t=2, halves=(0,))
         project(u - 1, halves=(1,))
         project(u, halves=(1,))
-        back_some(NACC)
+        back_some(len(to_back))
 
         weigh(LAST)
         for h in range(2):

@@ -46,7 +46,8 @@ THREE_QUARTER_END = 7
 BACK_START = TENSOR_END - 1
 BACK_PER_STEP = 4
 POOL_BLOCKS = 24
-LATE_EARLY = 3
+LATE_EARLY = 2
+EARLY_SHARES = 4
 WIDE_BUFS = {1: 5, 2: 6}
 
 
@@ -201,6 +202,7 @@ def tile_weighted_range_power_step_s13_kernel(
             return dst, src
 
         def interleave_on_gpsimd(u):
+            interleave_views(u - 1)
             interleave_views(u)
             src = unit_planes(u).rearrange("p j (n t) -> p n t j", t=PACK)
             dst = grouped[u][:].rearrange("p (t n j) -> p n t j", t=PACK, j=PACK)
@@ -219,8 +221,8 @@ def tile_weighted_range_power_step_s13_kernel(
         def omega_interleave(k):
             om_grouped[k] = work.tile([P, R * PACK], BF16, name="om_grouped", bufs=2, align_bytes=64)
             nc.vector.tensor_copy(
-                om_grouped[k][:].rearrange("p (c i j) -> p c j i", i=2, j=PACK),
-                om_raw[k][:].rearrange("p j (c i) -> p c j i", i=2),
+                om_grouped[k][:].rearrange("p (c i j) -> p c j i", i=PACK, j=PACK),
+                om_raw[k][:].rearrange("p j (c i) -> p c j i", i=PACK),
             )
 
         def omega_quantize(k):
@@ -409,12 +411,13 @@ def tile_weighted_range_power_step_s13_kernel(
         weigh(LAST - 1)
         scalar_share(first + 1)
         interleave_on_gpsimd(POOL_UNITS[LAST - 1])
-        quantize_and_project(first)
-        scalar_share(first + 2)
+        widen_next()
         quantize_v(LAST - 1)
         widen_unit(UNITS - 1)
+        scalar_share(first + 2)
         to_back.extend((tiles, LAST - 1) for tiles in RESIDENT)
-        back_some(NACC - 1)
+        back_some(EARLY_SHARES)
+        quantize_and_project(first)
         quantize_and_project(first + 1)
 
         u = UNITS - 1

@@ -42,10 +42,10 @@ POS = {gk: u for u, gk in enumerate(UNIT)}
 
 AHEAD = 2
 TENSOR_END = 15
-THREE_QUARTER_END = 7
+THREE_QUARTER_END = 8
 BACK_START = TENSOR_END - 1
 BACK_PER_STEP = 4
-POOL_BLOCKS = 24
+POOL_BLOCKS = 26
 LATE_EARLY = 2
 EARLY_SHARES = 4
 WIDE_BUFS = {1: 5, 2: 6}
@@ -204,8 +204,8 @@ def tile_weighted_range_power_step_s13_kernel(
         def interleave_on_gpsimd(u):
             interleave_views(u - 1)
             interleave_views(u)
-            src = unit_planes(u).rearrange("p j (n t) -> p n t j", t=PACK)
-            dst = grouped[u][:].rearrange("p (t n j) -> p n t j", t=PACK, j=PACK)
+            src = unit_planes(u).rearrange("p j (n t) -> p n j t", t=PACK)
+            dst = grouped[u][:].rearrange("p (t n j) -> p n j t", t=PACK, j=PACK)
             nc.gpsimd.tensor_scalar(dst[:, : 2 * POOL_BLOCKS], src[:, : 2 * POOL_BLOCKS], 1.0, 0.0, MULT, ADD)
 
         def new_codes(u):

@@ -92,8 +92,8 @@ def tile_weighted_range_power_step_s13_kernel(
         b_scales = keep.tile([P, NG, M], U8, name="b_scales", align_bytes=64)
         om_rows = keep.tile([P, MT, R], BF16, name="om_rows", align_bytes=64)
         a_sc_first = keep.tile([P, 1, PACK], F32, name="a_sc_first")
-        a_sc_rest = keep.tile([P, KG - 1, PACK], F32, name="a_sc_rest")
-        w_sb = keep.tile([P, NG, PACK], BF16, name="w_sb")
+        a_sc_rest = keep.tile([P, KG - 1, 2 * PACK], F32, name="a_sc_rest")
+        w_sb = keep.tile([P, NG, 4 * PACK], BF16, name="w_sb")
         noise_rows = keep.tile([P, P], BF16, name="noise_rows")
         ident = keep.tile([P, P], BF16, name="ident")
         neg_noise = keep.tile([P, MT], F32, name="neg_noise")
@@ -115,12 +115,14 @@ def tile_weighted_range_power_step_s13_kernel(
             nc.sync.dma_start(out=b_words[g][:], in_=at_words[g])
 
         nc.scalar.dma_start(out=a_sc_first[:], in_=a_sc_view[:, 0:1])
-        nc.scalar.dma_start(out=a_sc_rest[:], in_=a_sc_view[:, 1:KG])
+        nc.scalar.dma_start(out=a_sc_rest[:, :, 0:PACK], in_=a_sc_view[:, 1:KG])
         nc.vector.memset(warm[:, 0:1], 0.0)
         nc.scalar.activation(warm[:, 1:2], warm[:, 0:1], COPY, scale=-1.0)
-        nc.vector.memset(b_scales[:].rearrange("p g n -> p (g n)").bitcast(I32), 0)
-        nc.gpsimd.memset(noise_rows[:], 0.0)
-        make_identity(nc, ident[:])
+        nc.vector.memset(ident[:], 0.0)
+        make_identity(nc, ident[:], nomemset=True)
+        nc.vector.memset(noise_rows[:], 0.0)
+        nc.vector.memset(b_scales[:, 0:2].rearrange("p g n -> p (g n)").bitcast(I32), 0)
+        nc.vector.memset(b_scales[:, 2:NG].rearrange("p g n -> p (g n)").bitcast(I32), 0)
 
         for k in range(2):
             load_a(0, k, slice(0, 2))
@@ -135,7 +137,7 @@ def tile_weighted_range_power_step_s13_kernel(
         load_a(1, 2)
         load_om(3)
         load_a(1, 3)
-        nc.sync.dma_start(out=w_sb[:], in_=sample_w.rearrange("(g p j) -> p g j", p=P, j=PACK))
+        nc.sync.dma_start(out=w_sb[:, :, 0:PACK], in_=sample_w.rearrange("(g p j) -> p g j", p=P, j=PACK))
         load_a(2, 1)
         load_a(2, 3)
         load_a(3, 0)
@@ -250,7 +252,7 @@ def tile_weighted_range_power_step_s13_kernel(
                 nc.vector.tensor_tensor(
                     v_grouped[g][:, h, :].rearrange("p (c t) -> p c t", t=PACK),
                     z[g, h][:].rearrange("p t c -> p c t"),
-                    w_sb[:, g : g + 1, :].to_broadcast([P, P, PACK]),
+                    w_sb[:, g : g + 1, 0:PACK].to_broadcast([P, P, PACK]),
                     MULT,
                 )
 

@@ -137,9 +137,9 @@ def tile_weighted_range_power_step_s13_kernel(
         load_a(1, 2)
         load_om(3)
         load_a(1, 3)
-        nc.sync.dma_start(out=w_sb[:, :, 0:PACK], in_=sample_w.rearrange("(g p j) -> p g j", p=P, j=PACK))
         load_a(2, 1)
         load_a(2, 3)
+        nc.sync.dma_start(out=w_sb[:, :, 0:PACK], in_=sample_w.rearrange("(g p j) -> p g j", p=P, j=PACK))
         load_a(3, 0)
         load_a(3, 2)
         load_a(4, 1)

@@ -89,7 +89,7 @@ def tile_weighted_range_power_step_s13_kernel(
         v_codes = [keep.tile([P, R], U32, name="v_codes%d" % g, align_bytes=64) for g in range(NG)]
         v_scales = [keep.tile([P, R], U8, name="v_scales%d" % g, align_bytes=64) for g in range(NG)]
         b_words = [keep.tile([P, 2 * M], U8, name="b_words%d" % g, align_bytes=64) for g in range(NG)]
-        b_scales = keep.tile([P, NG, M], U8, name="b_scales", align_bytes=64)
+        b_scales = keep.tile([P, NG * M], U8, name="b_scales", align_bytes=64)
         om_rows = keep.tile([P, MT, R], BF16, name="om_rows", align_bytes=64)
         a_sc_first = keep.tile([P, 1, PACK], F32, name="a_sc_first")
         a_sc_rest = keep.tile([P, KG - 1, 2 * PACK], F32, name="a_sc_rest")
@@ -121,8 +121,6 @@ def tile_weighted_range_power_step_s13_kernel(
         nc.vector.memset(ident[:], 0.0)
         make_identity(nc, ident[:], nomemset=True)
         nc.vector.memset(noise_rows[:], 0.0)
-        nc.vector.memset(b_scales[:, 0:2].rearrange("p g n -> p (g n)").bitcast(I32), 0)
-        nc.vector.memset(b_scales[:, 2:NG].rearrange("p g n -> p (g n)").bitcast(I32), 0)
 
         for k in range(2):
             load_a(0, k, slice(0, 2))
@@ -144,17 +142,20 @@ def tile_weighted_range_power_step_s13_kernel(
         load_a(3, 2)
         load_a(4, 1)
         nc.sync.dma_start(out=noise_rows[0:MT, :], in_=noise_var.rearrange("(m p) -> m p", p=P))
-        for q in range(4):
-            nc.sync.dma_start(out=b_scales[q:P:32].bitcast(I32), in_=b_sc_view[q:16:4])
         load_b(0)
         load_b(1)
         load_a(4, 3)
         load_b(2)
         load_a(5, 0)
         load_a(5, 2)
-        for g in range(3, NG):
-            load_b(g)
-        nc.sync.dma_start(out=om_rows[:], in_=omega.rearrange("(m p) r -> p m r", p=P))
+
+        def load_rest():
+            for q in range(4):
+                rows = b_scales[q:P:32].bitcast(I32).rearrange("q (g n) -> q g n", g=NG)
+                nc.sync.dma_start(out=rows, in_=b_sc_view[q:16:4])
+            for g in range(3, NG):
+                load_b(g)
+            nc.sync.dma_start(out=om_rows[:], in_=omega.rearrange("(m p) r -> p m r", p=P))
 
         planes, side, grouped, a_codes, a_scales = {}, {}, {}, {}, {}
         om_grouped, z, v_grouped, acc, y, y_half = {}, {}, {}, {}, {}, {}
@@ -211,7 +212,10 @@ def tile_weighted_range_power_step_s13_kernel(
             nc.gpsimd.tensor_scalar(dst[:, : 2 * POOL_BLOCKS], src[:, : 2 * POOL_BLOCKS], 1.0, 0.0, MULT, ADD)
 
         def new_codes(u):
-            a_codes[u] = work.tile([P, S], U32, name="codes", bufs=6, align_bytes=64)
+            if u < NG:
+                a_codes[u] = b_scales[:, M * u : M * (u + 1)].bitcast(U32)
+            else:
+                a_codes[u] = work.tile([P, S], U32, name="codes", bufs=6, align_bytes=64)
             a_scales[u] = work.tile([P, S], U8, name="scales", bufs=6, align_bytes=64)
 
         def quantize_a(u, t0=0, t1=PACK):
@@ -273,7 +277,7 @@ def tile_weighted_range_power_step_s13_kernel(
                 nc.tensor.matmul_mx(
                     out=acc[tiles][:, i, c : c + width],
                     lhsT=b_words[g][:, 2 * P * m : 2 * P * (m + 1)].bitcast(FP4X4),
-                    lhsT_scale=b_scales[:, g, P * m : P * (m + 1)],
+                    lhsT_scale=b_scales[:, M * g + P * m : M * g + P * (m + 1)],
                     rhs=v_codes[g][:, c : c + width].bitcast(FP8X4),
                     rhs_scale=v_scales[g][:, c : c + width],
                     start=(g == 0 and (c, i, m) == passes[0]),
@@ -392,6 +396,8 @@ def tile_weighted_range_power_step_s13_kernel(
                     project(u, halves=(h,))
             for u in due:
                 to_project.remove(u)
+            if NG - 1 in due:
+                load_rest()
             if not ready:
                 tensor_other(s)
 

@@ -34,11 +34,18 @@ RESIDENT = [(2 * b, 2 * b + 1) for b in range(NACC)]
 LATE = [(12, 13), (14,), (15,)]
 BANK_OF = dict([(tiles, "acc%d" % b) for b, tiles in enumerate(RESIDENT)] + list(zip(LATE, ("z0", "z1", "acc0"))))
 
-SPANS = (((0,), (1, 2), (3, 4), (5,)), ((0,), (1,), (2, 3), (4, 5)))
+SPANS = (((0, 1), (2,), (3, 4), (5,)), ((0, 1), (2, 3), (4, 5)))
 SPAN_OF = {(g, k): span for k in range(KG) for span in SPANS[k % 2] for g in span}
 
-UNIT = [(g, k) for g in range(LAST) for k in range(KG)] + [(LAST, k) for k in (1, 3, 0, 2)]
+UNIT = (
+    [(g, k) for k in range(KG) for g in range(2)]
+    + [(g, k) for g in range(2, LAST) for k in range(KG)]
+    + [(LAST, k) for k in (1, 3, 0, 2)]
+)
 POS = {gk: u for u, gk in enumerate(UNIT)}
+FIRST_OF = [min(POS[g, k] for k in range(KG)) for g in range(NG)]
+LAST_OF = [max(POS[g, k] for k in range(KG)) for g in range(NG)]
+PARKED = [POS[0, k] for k in range(KG)] + [POS[1, 0], POS[1, 1]]
 
 AHEAD = 2
 TENSOR_END = 15
@@ -48,12 +55,11 @@ BACK_PER_STEP = 4
 POOL_BLOCKS = 26
 LATE_EARLY = 2
 EARLY_SHARES = 4
-WIDE_BUFS = {1: 5, 2: 6}
+WIDE_BUFS = {1: 3, 2: 7}
 
 
 def weigh_step(g):
-    step = KG * (g + 1) + AHEAD
-    return step + 1 if step <= BACK_START else step
+    return LAST_OF[g] + AHEAD + 1 + (1 if g in (1, 2) else 0)
 
 
 POOL_UNITS = [weigh_step(g) + AHEAD for g in range(LAST - 2)] + [KG * LAST - 1, UNITS - 2]
@@ -61,9 +67,9 @@ POOL_UNITS = [weigh_step(g) + AHEAD for g in range(LAST - 2)] + [KG * LAST - 1, 
 
 def on_scalar(g, k, j):
     u = POS[g, k]
-    if u < AHEAD:
+    if u == 0:
         return j == 1
-    if u == KG - 1:
+    if (g, k) == (2, 2):
         return j >= PACK - 2
     return j == PACK - 1 and u < TENSOR_END and u not in POOL_UNITS
 
@@ -115,27 +121,26 @@ def tile_weighted_range_power_step_s13_kernel(
             nc.sync.dma_start(out=b_words[g][:], in_=at_words[g])
 
         nc.scalar.dma_start(out=a_sc_first[:], in_=a_sc_view[:, 0:1])
-        nc.scalar.dma_start(out=a_sc_rest[:, :, 0:PACK], in_=a_sc_view[:, 1:KG])
         nc.vector.memset(warm[:, 0:1], 0.0)
         nc.scalar.activation(warm[:, 1:2], warm[:, 0:1], COPY, scale=-1.0)
+        nc.scalar.dma_start(out=a_sc_rest[:, :, 0:PACK], in_=a_sc_view[:, 1:KG])
         nc.vector.memset(ident[:], 0.0)
         make_identity(nc, ident[:], nomemset=True)
         nc.vector.memset(noise_rows[:], 0.0)
 
-        for k in range(2):
-            load_a(0, k, slice(0, 2))
-            load_a(0, k, slice(2, 4))
-        load_a(0, 2)
+        for j in range(PACK):
+            load_a(0, 0, slice(j, j + 1))
         load_om(0)
-        load_a(0, 3)
+        load_a(0, 1, slice(0, 2))
+        load_a(0, 1, slice(2, 4))
         load_om(1)
-        load_a(1, 0)
-        load_a(1, 1)
+        load_a(0, 2)
         load_om(2)
-        load_a(1, 2)
+        load_a(0, 3)
         load_om(3)
-        load_a(1, 3)
+        load_a(2, 0)
         load_a(2, 1)
+        load_a(2, 2)
         load_a(2, 3)
         nc.sync.dma_start(out=w_sb[:, :, 0:PACK], in_=sample_w.rearrange("(g p j) -> p g j", p=P, j=PACK))
         load_a(3, 0)
@@ -160,18 +165,18 @@ def tile_weighted_range_power_step_s13_kernel(
         planes, side, grouped, a_codes, a_scales = {}, {}, {}, {}, {}
         om_grouped, z, v_grouped, acc, y, y_half = {}, {}, {}, {}, {}, {}
 
-        def widen(g, k, j):
+        def widen(g, k, j, cols=slice(None)):
             if (g, k) not in planes:
                 width = len(SPAN_OF[g, k])
                 planes[g, k] = work.tile(
                     [P, PACK, S * width], BF16, name="wide%d" % width, bufs=WIDE_BUFS[width], align_bytes=64
                 )
-            in_ = a_raw[g, k][:, j, :].bitcast(FP8)
+            in_ = a_raw[g, k][:, j, cols].bitcast(FP8)
             scale = a_sc_first[:, 0, j : j + 1] if k == 0 else a_sc_rest[:, k - 1, j : j + 1]
             if on_scalar(g, k, j):
-                nc.scalar.activation(planes[g, k][:, j, :], in_, COPY, scale=scale)
+                nc.scalar.activation(planes[g, k][:, j, cols], in_, COPY, scale=scale)
             else:
-                nc.vector.tensor_scalar(planes[g, k][:, j, :], in_, scale, None, MULT)
+                nc.vector.tensor_scalar(planes[g, k][:, j, cols], in_, scale, None, MULT)
 
         def unit_planes(u):
             g, k = UNIT[u]
@@ -212,11 +217,11 @@ def tile_weighted_range_power_step_s13_kernel(
             nc.gpsimd.tensor_scalar(dst[:, : 2 * POOL_BLOCKS], src[:, : 2 * POOL_BLOCKS], 1.0, 0.0, MULT, ADD)
 
         def new_codes(u):
-            if u < NG:
-                a_codes[u] = b_scales[:, M * u : M * (u + 1)].bitcast(U32)
+            if u in PARKED:
+                a_codes[u] = b_scales[:, M * PARKED.index(u) : M * (PARKED.index(u) + 1)].bitcast(U32)
             else:
                 a_codes[u] = work.tile([P, S], U32, name="codes", bufs=6, align_bytes=64)
-            a_scales[u] = work.tile([P, S], U8, name="scales", bufs=6, align_bytes=64)
+            a_scales[u] = work.tile([P, S], U8, name="scales", bufs=10, align_bytes=64)
 
         def quantize_a(u, t0=0, t1=PACK):
             cols = slice(P * t0, P * t1)
@@ -237,7 +242,7 @@ def tile_weighted_range_power_step_s13_kernel(
         def project(u, ts=range(PACK), closing_t=PACK - 1, halves=range(2)):
             g, k = UNIT[u]
             for h in halves:
-                if u % KG == 0:
+                if u == FIRST_OF[g]:
                     z[g, h] = psum.tile([P, PACK, P], F32, name="z%d_%d" % (g, h), tag="z%d" % h)
                 for t in ts:
                     nc.tensor.matmul_mx(
@@ -246,8 +251,8 @@ def tile_weighted_range_power_step_s13_kernel(
                         lhsT_scale=a_scales[u][:, P * t : P * (t + 1)],
                         rhs=om_codes[k][:, P * h : P * (h + 1)].bitcast(FP8X4),
                         rhs_scale=om_scales[k][:, P * h : P * (h + 1)],
-                        start=(u % KG == 0 and t == 0),
-                        stop=(u % KG == KG - 1 and t == closing_t),
+                        start=(u == FIRST_OF[g] and t == 0),
+                        stop=(u == LAST_OF[g] and t == closing_t),
                     )
 
         def weigh(g):
@@ -285,7 +290,7 @@ def tile_weighted_range_power_step_s13_kernel(
                 )
 
         def noise_onto_partitions():
-            noise_t = psum.tile([P, P], BF16, name="noise_t", tag=borrow_bank(BACK_START))
+            noise_t = psum.tile([P, P], BF16, name="noise_t", tag=borrow_bank(BACK_START + 1))
             nc.tensor.transpose(noise_t[:], noise_rows[:], ident[:])
             return noise_t
 
@@ -319,7 +324,7 @@ def tile_weighted_range_power_step_s13_kernel(
                 opens = POS[g, k]
                 if opens == u == POOL_UNITS[LAST - 2] and j == PACK - 1:
                     break
-                if opens > u + 1 or (opens == u + 1 and (len(SPAN_OF[g, k]) == 1 or j >= PACK // 2 or opens == KG)):
+                if opens > u + 1 or (opens == u + 1 and (len(SPAN_OF[g, k]) == 1 or j >= PACK // 2)):
                     break
                 widen(*to_widen.pop(0))
 
@@ -354,22 +359,33 @@ def tile_weighted_range_power_step_s13_kernel(
             if s >= BACK_START:
                 back_some(BACK_PER_STEP, s)
 
-        widen_for(AHEAD - 1)
+        for j0 in (0, 1):
+            for g in range(2):
+                widen(0, 0, j0, slice(S * g, S * (g + 1)))
+        for g in range(2):
+            for j in (2, 3):
+                widen(0, 0, j, slice(S * g, S * (g + 1)))
+        to_widen[:PACK] = []
+        omega_interleave(0)
         for u in range(AHEAD):
             interleave_on_tensor(u)
         for s in range(UNITS - KG):
-            scalar_share(s)
-            scalar_widen_for(s + AHEAD + min(s, 1))
+            for u in {0: (0, 1), 1: ()}.get(s, (s,)):
+                scalar_share(u)
+            scalar_widen_for(s + AHEAD + 1)
             for q0, q1, bank in side.get(s, ()):
                 nc.scalar.copy(
                     grouped[s][:].rearrange("p (t m j) -> p t m j", t=PACK, j=PACK)[:, :, 32 * q0 : 32 * q1, :],
                     bank[:],
                 )
-            if s == BACK_START:
+            if s == BACK_START + 1:
                 nc.scalar.activation(neg_noise[:], noise_t[:, 0:MT], COPY, scale=-1.0)
             ready = [g for g in range(LAST) if weigh_step(g) == s]
-            if 1 <= s <= KG:
-                omega_interleave(s - 1)
+            omega_pass = [k for k in range(1, KG) if POS[0, k] == s + 1]
+            for k in omega_pass:
+                omega_interleave(k)
+            if weigh_step(0) - AHEAD <= s <= weigh_step(0):
+                widen_next()
             if s >= AHEAD:
                 new_codes(s - AHEAD)
                 quantize_a(s - AHEAD)
@@ -384,21 +400,22 @@ def tile_weighted_range_power_step_s13_kernel(
                 weigh(g)
                 interleave_on_gpsimd(POOL_UNITS[g])
             widen_for(s + AHEAD)
-            if 1 <= s <= KG:
-                omega_quantize(s - 1)
+            for k in [0] * (s == 0) + omega_pass:
+                omega_quantize(k)
             if s == BACK_START - 1:
                 noise_t = noise_onto_partitions()
-            if ready:
+            other_first = ready or s + AHEAD == TENSOR_END - 1
+            if other_first:
                 tensor_other(s)
-            due = [u for u in to_project if u <= s - AHEAD and u // KG <= len(v_grouped)]
+            due = [u for u in to_project if u <= s - AHEAD and UNIT[u][0] <= len(v_grouped)]
             for h in range(2):
                 for u in due:
                     project(u, halves=(h,))
             for u in due:
                 to_project.remove(u)
-            if NG - 1 in due:
+            if PARKED[-1] in due:
                 load_rest()
-            if not ready:
+            if not other_first:
                 tensor_other(s)
 
         first = UNITS - KG

@@ -102,6 +102,7 @@ def tile_weighted_range_power_step_s13_kernel(
         w_sb = keep.tile([P, NG, 4 * PACK], BF16, name="w_sb")
         noise_rows = keep.tile([P, P], BF16, name="noise_rows")
         ident = keep.tile([P, P], BF16, name="ident")
+        w_last = keep.tile([P, P, PACK], BF16, name="w_last", align_bytes=64)
         neg_noise = keep.tile([P, MT], F32, name="neg_noise")
         warm = keep.tile([P, 2], F32, name="warm")
 
@@ -256,12 +257,13 @@ def tile_weighted_range_power_step_s13_kernel(
                     )
 
         def weigh(g):
+            weights = w_last[:] if g == LAST else w_sb[:, g : g + 1, 0:PACK].to_broadcast([P, P, PACK])
             v_grouped[g] = work.tile([P, 2, P * PACK], BF16, name="v_grouped", bufs=2, align_bytes=64)
             for h in range(2):
                 nc.vector.tensor_tensor(
                     v_grouped[g][:, h, :].rearrange("p (c t) -> p c t", t=PACK),
                     z[g, h][:].rearrange("p t c -> p c t"),
-                    w_sb[:, g : g + 1, 0:PACK].to_broadcast([P, P, PACK]),
+                    weights,
                     MULT,
                 )
 
@@ -449,6 +451,7 @@ def tile_weighted_range_power_step_s13_kernel(
         dst, src = interleave_views(u)
         nc.scalar.copy(dst[:, :, 0:2], src[:, :, 0:2])
         nc.scalar.copy(dst[:, :, 2:3], src[:, :, 2:3])
+        nc.scalar.copy(w_last[:], w_sb[:, LAST:NG, 0:PACK].to_broadcast([P, P, PACK]))
         for tiles in RESIDENT + LATE:
             noise_term(tiles)
         nc.vector.tensor_copy(dst[:, :, 3:4], src[:, :, 3:4])

from contextlib import ExitStack

import concourse.mybir as mybir
from concourse.masks import make_identity

M, N, R = 2048, 3072, 256
FLOPS = 2 * 2 * M * N * R

F32 = mybir.dt.float32
BF16 = mybir.dt.bfloat16
U32 = mybir.dt.uint32
I32 = mybir.dt.int32
U8 = mybir.dt.uint8
FP8 = mybir.dt.float8_e4m3fn
FP8X4 = mybir.dt.float8_e4m3fn_x4
FP4X4 = mybir.dt.float4_e2m1fn_x4
MULT = mybir.AluOpType.mult
ADD = mybir.AluOpType.add
COPY = mybir.ActivationFunctionType.Copy

P = 128
PACK = 4
S = 512
KG = M // 512
NG = N // S
LAST = NG - 1
UNITS = NG * KG
BLOCKS = S // 8
QUARTER = BLOCKS // 4
MT = M // P

NACC = 6
RESIDENT = [(2 * b, 2 * b + 1) for b in range(NACC)]
LATE = [(12, 13), (14,), (15,)]
BANK_OF = dict([(tiles, "acc%d" % b) for b, tiles in enumerate(RESIDENT)] + list(zip(LATE, ("z0", "z1", "acc0"))))

SPANS = (((0, 1), (2,), (3, 4), (5,)), ((0, 1), (2, 3), (4, 5)))
SPAN_OF = {(g, k): span for k in range(KG) for span in SPANS[k % 2] for g in span}

UNIT = (
    [(g, k) for k in range(KG) for g in range(2)]
    + [(g, k) for g in range(2, LAST) for k in range(KG)]
    + [(LAST, k) for k in (1, 3, 0, 2)]
)
POS = {gk: u for u, gk in enumerate(UNIT)}
FIRST_OF = [min(POS[g, k] for k in range(KG)) for g in range(NG)]
LAST_OF = [max(POS[g, k] for k in range(KG)) for g in range(NG)]
PARKED = [POS[0, k] for k in range(KG)] + [POS[1, 0], POS[1, 1]]

AHEAD = 2
TENSOR_END = 15
THREE_QUARTER_END = 8
BACK_START = TENSOR_END - 1
BACK_PER_STEP = 4
POOL_BLOCKS = 26
LATE_EARLY = 2
EARLY_SHARES = 4
WIDE_BUFS = {1: 3, 2: 7}


def weigh_step(g):
    return LAST_OF[g] + AHEAD + 1 + (1 if g in (1, 2) else 0)


POOL_UNITS = [weigh_step(g) + AHEAD for g in range(LAST - 2)] + [KG * LAST - 1, UNITS - 2]


def on_scalar(g, k, j):
    u = POS[g, k]
    if u == 0:
        return j == 1
    if (g, k) == (2, 2):
        return j >= PACK - 2
    return j == PACK - 1 and u < TENSOR_END and u not in POOL_UNITS


def tile_weighted_range_power_step_s13_kernel(
    tc, a_bytes, a_scale, omega, sample_w, noise_var, at_words, at_scales, out
):
    nc = tc.nc
    with ExitStack() as ctx:
        keep = ctx.enter_context(tc.tile_pool(name="keep", bufs=1))
        work = ctx.enter_context(tc.tile_pool(name="work", bufs=3))
        psum = ctx.enter_context(tc.psum_pool(name="psum", bufs=1))
        ctx.enter_context(tc.manual_schedule())

        a_raw = {
            (span[0], k): keep.tile([P, PACK, S * len(span)], U8, name="a_raw%d_%d" % (span[0], k), align_bytes=64)
            for k in range(KG)
            for span in SPANS[k % 2]
        }
        om_raw = [keep.tile([P, PACK, R], BF16, name="om_raw%d" % k, align_bytes=64) for k in range(KG)]
        om_codes = [keep.tile([P, R], U32, name="om_codes%d" % k, align_bytes=64) for k in range(KG)]
        om_scales = [keep.tile([P, R], U8, name="om_scales%d" % k, align_bytes=64) for k in range(KG)]
        v_codes = [keep.tile([P, R], U32, name="v_codes%d" % g, align_bytes=64) for g in range(NG)]
        v_scales = [keep.tile([P, R], U8, name="v_scales%d" % g, align_bytes=64) for g in range(NG)]
        b_words = [keep.tile([P, 2 * M], U8, name="b_words%d" % g, align_bytes=64) for g in range(NG)]
        b_scales = keep.tile([P, NG * M], U8, name="b_scales", align_bytes=64)
        om_rows = keep.tile([P, MT, R], BF16, name="om_rows", align_bytes=64)
        a_sc_first = keep.tile([P, 1, PACK], F32, name="a_sc_first")
        a_sc_rest = keep.tile([P, KG - 1, 2 * PACK], F32, name="a_sc_rest")
        w_sb = keep.tile([P, NG, 4 * PACK], BF16, name="w_sb")
        noise_rows = keep.tile([P, P], BF16, name="noise_rows")
        ident = keep.tile([P, P], BF16, name="ident")
        w_last = keep.tile([P, P, PACK], BF16, name="w_last", align_bytes=64)
        neg_noise = keep.tile([P, MT], F32, name="neg_noise")
        warm = keep.tile([P, 2], F32, name="warm")

        a_view = a_bytes.rearrange("(k p j) n -> k p j n", p=P, j=PACK)
        a_sc_view = a_scale.rearrange("(k p j) o -> p k (j o)", p=P, j=PACK)
        om_view = omega.rearrange("(k p j) r -> k p j r", p=P, j=PACK)
        b_sc_view = at_scales.bitcast(I32).rearrange("g q n -> q g n")

        def load_a(g, k, rows=slice(0, PACK)):
            cols = slice(S * g, S * (g + len(SPAN_OF[g, k])))
            nc.sync.dma_start(out=a_raw[g, k][:, rows, :], in_=a_view[k][:, rows, cols])

        def load_om(k):
            nc.sync.dma_start(out=om_raw[k][:], in_=om_view[k])

        def load_b(g):
            nc.sync.dma_start(out=b_words[g][:], in_=at_words[g])

        nc.scalar.dma_start(out=a_sc_first[:], in_=a_sc_view[:, 0:1])
        nc.vector.memset(warm[:, 0:1], 0.0)
        nc.scalar.activation(warm[:, 1:2], warm[:, 0:1], COPY, scale=-1.0)
        nc.scalar.dma_start(out=a_sc_rest[:, :, 0:PACK], in_=a_sc_view[:, 1:KG])
        nc.vector.memset(ident[:], 0.0)
        make_identity(nc, ident[:], nomemset=True)
        nc.vector.memset(noise_rows[:], 0.0)

        for j in range(PACK):
            load_a(0, 0, slice(j, j + 1))
        load_om(0)
        load_a(0, 1, slice(0, 2))
        load_a(0, 1, slice(2, 4))
        load_om(1)
        load_a(0, 2)
        load_om(2)
        load_a(0, 3)
        load_om(3)
        load_a(2, 0)
        load_a(2, 1)
        load_a(2, 2)
        load_a(2, 3)
        nc.sync.dma_start(out=w_sb[:, :, 0:PACK], in_=sample_w.rearrange("(g p j) -> p g j", p=P, j=PACK))
        load_a(3, 0)
        load_a(3, 2)
        load_a(4, 1)
        nc.sync.dma_start(out=noise_rows[0:MT, :], in_=noise_var.rearrange("(m p) -> m p", p=P))
        load_b(0)
        load_b(1)
        load_a(4, 3)
        load_b(2)
        load_a(5, 0)
        load_a(5, 2)

        def load_rest():
            for q in range(4):
                rows = b_scales[q:P:32].bitcast(I32).rearrange("q (g n) -> q g n", g=NG)
                nc.sync.dma_start(out=rows, in_=b_sc_view[q:16:4])
            for g in range(3, NG):
                load_b(g)
            nc.sync.dma_start(out=om_rows[:], in_=omega.rearrange("(m p) r -> p m r", p=P))

        planes, side, grouped, a_codes, a_scales = {}, {}, {}, {}, {}
        om_grouped, z, v_grouped, acc, y, y_half = {}, {}, {}, {}, {}, {}

        def widen(g, k, j, cols=slice(None)):
            if (g, k) not in planes:
                width = len(SPAN_OF[g, k])
                planes[g, k] = work.tile(
                    [P, PACK, S * width], BF16, name="wide%d" % width, bufs=WIDE_BUFS[width], align_bytes=64
                )
            in_ = a_raw[g, k][:, j, cols].bitcast(FP8)
            scale = a_sc_first[:, 0, j : j + 1] if k == 0 else a_sc_rest[:, k - 1, j : j + 1]
            if on_scalar(g, k, j):
                nc.scalar.activation(planes[g, k][:, j, cols], in_, COPY, scale=scale)
            else:
                nc.vector.tensor_scalar(planes[g, k][:, j, cols], in_, scale, None, MULT)

        def unit_planes(u):
            g, k = UNIT[u]
            first = SPAN_OF[g, k][0]
            return planes[first, k][:, :, S * (g - first) : S * (g - first + 1)]

        def borrow_bank(step):
            b = lent_until.index(min(lent_until))
            lent_until[b] = step
            return "acc%d" % b

        def interleave_on_tensor(u):
            side[u] = []
            for q0, q1 in ((2, 4), (1, 2)) if AHEAD <= u < THREE_QUARTER_END else ((2, 4),):
                bank = psum.tile([P, PACK, 32 * (q1 - q0), PACK], BF16, name="side", tag=borrow_bank(u))
                side[u].append((q0, q1, bank))
                for q in range(q0, q1):
                    nc.tensor.matmul(
                        bank[:, :, 32 * (q - q0) : 32 * (q - q0 + 1), :].rearrange("p t m j -> p j m t"),
                        lhsT=ident[:],
                        rhs=unit_planes(u)[:, :, P * q : P * (q + 1)],
                        start=True,
                        stop=True,
                    )

        def interleave_views(u):
            if u not in grouped:
                grouped[u] = work.tile([P, S * PACK], BF16, name="grouped", bufs=AHEAD + 2, align_bytes=64)
            src = unit_planes(u).rearrange("p j (m i t) -> p m t j i", i=2, t=PACK)
            dst = grouped[u][:].rearrange("p (t m i j) -> p m t j i", t=PACK, i=2, j=PACK)
            return dst, src

        def interleave_on_gpsimd(u):
            interleave_views(u - 1)
            interleave_views(u)
            src = unit_planes(u).rearrange("p j (n t) -> p n j t", t=PACK)
            dst = grouped[u][:].rearrange("p (t n j) -> p n j t", t=PACK, j=PACK)
            nc.gpsimd.tensor_scalar(dst[:, : 2 * POOL_BLOCKS], src[:, : 2 * POOL_BLOCKS], 1.0, 0.0, MULT, ADD)

        def new_codes(u):
            if u in PARKED:
                a_codes[u] = b_scales[:, M * PARKED.index(u) : M * (PARKED.index(u) + 1)].bitcast(U32)
            else:
                a_codes[u] = work.tile([P, S], U32, name="codes", bufs=6, align_bytes=64)
            a_scales[u] = work.tile([P, S], U8, name="scales", bufs=10, align_bytes=64)

        def quantize_a(u, t0=0, t1=PACK):
            cols = slice(P * t0, P * t1)
            nc.vector.quantize_mx(
                a_codes[u][:, cols].bitcast(FP8X4), a_scales[u][:, cols], grouped[u][:, S * t0 : S * t1]
            )

        def omega_interleave(k):
            om_grouped[k] = work.tile([P, R * PACK], BF16, name="om_grouped", bufs=2, align_bytes=64)
            nc.vector.tensor_copy(
                om_grouped[k][:].rearrange("p (c i j) -> p c j i", i=PACK, j=PACK),
                om_raw[k][:].rearrange("p j (c i) -> p c j i", i=PACK),
            )

        def omega_quantize(k):
            nc.vector.quantize_mx(om_codes[k][:].bitcast(FP8X4), om_scales[k][:], om_grouped[k][:])

        def project(u, ts=range(PACK), closing_t=PACK - 1, halves=range(2)):
            g, k = UNIT[u]
            for h in halves:
                if u == FIRST_OF[g]:
                    z[g, h] = psum.tile([P, PACK, P], F32, name="z%d_%d" % (g, h), tag="z%d" % h)
                for t in ts:
                    nc.tensor.matmul_mx(
                        out=z[g, h][:, t, :],
                        lhsT=a_codes[u][:, P * t : P * (t + 1)].bitcast(FP8X4),
                        lhsT_scale=a_scales[u][:, P * t : P * (t + 1)],
                        rhs=om_codes[k][:, P * h : P * (h + 1)].bitcast(FP8X4),
                        rhs_scale=om_scales[k][:, P * h : P * (h + 1)],
                        start=(u == FIRST_OF[g] and t == 0),
                        stop=(u == LAST_OF[g] and t == closing_t),
                    )

        def weigh(g):
            weights = w_last[:] if g == LAST else w_sb[:, g : g + 1, 0:PACK].to_broadcast([P, P, PACK])
            v_grouped[g] = work.tile([P, 2, P * PACK], BF16, name="v_grouped", bufs=2, align_bytes=64)
            for h in range(2):
                nc.vector.tensor_tensor(
                    v_grouped[g][:, h, :].rearrange("p (c t) -> p c t", t=PACK),
                    z[g, h][:].rearrange("p t c -> p c t"),
                    weights,
                    MULT,
                )

        def quantize_v(g, h0=0, h1=2):
            cols = slice(P * h0, P * h1)
            nc.vector.quantize_mx(
                v_codes[g][:, cols].bitcast(FP8X4),
                v_scales[g][:, cols],
                v_grouped[g][:, h0:h1, :].rearrange("p h c -> p (h c)"),
            )

        def back(tiles, g):
            if g == 0:
                acc[tiles] = psum.tile([P, len(tiles), R], F32, name="acc%d" % tiles[0], tag=BANK_OF[tiles])
            width = P if (tiles, g) == (RESIDENT[0], LAST) else R
            passes = [(c, i, m) for c in range(0, R, width) for i, m in enumerate(tiles)]
            for c, i, m in passes:
                nc.tensor.matmul_mx(
                    out=acc[tiles][:, i, c : c + width],
                    lhsT=b_words[g][:, 2 * P * m : 2 * P * (m + 1)].bitcast(FP4X4),
                    lhsT_scale=b_scales[:, M * g + P * m : M * g + P * (m + 1)],
                    rhs=v_codes[g][:, c : c + width].bitcast(FP8X4),
                    rhs_scale=v_scales[g][:, c : c + width],
                    start=(g == 0 and (c, i, m) == passes[0]),
                    stop=(g == LAST and (c, i, m) == passes[-1]),
                )

        def noise_onto_partitions():
            noise_t = psum.tile([P, P], BF16, name="noise_t", tag=borrow_bank(BACK_START + 1))
            nc.tensor.transpose(noise_t[:], noise_rows[:], ident[:])
            return noise_t

        out_view = out.rearrange("(m p) r -> p m r", p=P)

        def noise_term(tiles):
            half = tiles[0] // (MT // 2)
            if half not in y_half:
                y_half[half] = work.tile(
                    [P, MT // 2, R], F32, name="y%d" % half, tag="wide2", bufs=WIDE_BUFS[2], align_bytes=64
                )
            y[tiles] = y_half[half][:, tiles[0] % (MT // 2) : tiles[0] % (MT // 2) + len(tiles), :]
            for i, m in enumerate(tiles):
                nc.scalar.activation(y[tiles][:, i, :], om_rows[:, m, :], COPY, scale=neg_noise[:, m : m + 1])

        def finish(tiles):
            parts = [(0, 1), (1, 2)] if tiles == RESIDENT[0] else [(0, len(tiles))]
            for i0, i1 in parts:
                part = y[tiles][:, i0:i1, :]
                nc.vector.tensor_tensor(part, acc[tiles][:, i0:i1, :], part, ADD)
                nc.sync.dma_start(out=out_view[:, tiles[0] + i0 : tiles[0] + i1, :], in_=part)

        to_widen = [(g, k, j) for g, k in UNIT if SPAN_OF[g, k][0] == g for j in range(PACK)]
        to_project = list(range(UNITS))
        to_back = []
        lent_until = [b - NACC for b in range(NACC)]

        def widen_for(u):
            while to_widen:
                g, k, j = to_widen[0]
                opens = POS[g, k]
                if opens == u == POOL_UNITS[LAST - 2] and j == PACK - 1:
                    break
                if opens > u + 1 or (opens == u + 1 and (len(SPAN_OF[g, k]) == 1 or j >= PACK // 2)):
                    break
                widen(*to_widen.pop(0))

        def widen_unit(u):
            while to_widen and POS[to_widen[0][:2]] <= u:
                widen(*to_widen.pop(0))

        def widen_next():
            item = [x for x in to_widen if not on_scalar(*x)][0]
            to_widen.remove(item)
            widen(*item)

        def scalar_widen_for(u):
            for item in [x for x in to_widen if on_scalar(*x) and POS[x[:2]] <= u]:
                to_widen.remove(item)
                widen(*item)

        def back_some(count, s=UNITS):
            for item in [x for x in to_back if lent_until[RESIDENT.index(x[0])] <= s][:count]:
                back(*item)
                to_back.remove(item)

        def scalar_share(u):
            dst, src = interleave_views(u)
            lo = POOL_BLOCKS if u in POOL_UNITS else 0
            hi = QUARTER * side[u][-1][0] if u in side else BLOCKS
            nc.scalar.copy(dst[:, lo:hi], src[:, lo:hi])

        def tensor_other(s):
            if s + AHEAD < TENSOR_END:
                interleave_on_tensor(s + AHEAD)
            if s >= BACK_START:
                back_some(BACK_PER_STEP, s)

        for j0 in (0, 1):
            for g in range(2):
                widen(0, 0, j0, slice(S * g, S * (g + 1)))
        for g in range(2):
            for j in (2, 3):
                widen(0, 0, j, slice(S * g, S * (g + 1)))
        to_widen[:PACK] = []
        omega_interleave(0)
        for u in range(AHEAD):
            interleave_on_tensor(u)
        for s in range(UNITS - KG):
            for u in {0: (0, 1), 1: ()}.get(s, (s,)):
                scalar_share(u)
            scalar_widen_for(s + AHEAD + 1)
            for q0, q1, bank in side.get(s, ()):
                nc.scalar.copy(
                    grouped[s][:].rearrange("p (t m j) -> p t m j", t=PACK, j=PACK)[:, :, 32 * q0 : 32 * q1, :],
                    bank[:],
                )
            if s == BACK_START + 1:
                nc.scalar.activation(neg_noise[:], noise_t[:, 0:MT], COPY, scale=-1.0)
            ready = [g for g in range(LAST) if weigh_step(g) == s]
            omega_pass = [k for k in range(1, KG) if POS[0, k] == s + 1]
            for k in omega_pass:
                omega_interleave(k)
            if weigh_step(0) - AHEAD <= s <= weigh_step(0):
                widen_next()
            if s >= AHEAD:
                new_codes(s - AHEAD)
                quantize_a(s - AHEAD)
            for g in range(LAST):
                if weigh_step(g) == s - 1:
                    quantize_v(g)
                    if g < LAST - 2:
                        to_back.extend((tiles, g) for tiles in RESIDENT)
            for g in ready:
                widen_unit(s + AHEAD)
                widen_next()
                weigh(g)
                interleave_on_gpsimd(POOL_UNITS[g])
            widen_for(s + AHEAD)
            for k in [0] * (s == 0) + omega_pass:
                omega_quantize(k)
            if s == BACK_START - 1:
                noise_t = noise_onto_partitions()
            other_first = ready or s + AHEAD == TENSOR_END - 1
            if other_first:
                tensor_other(s)
            due = [u for u in to_project if u <= s - AHEAD and UNIT[u][0] <= len(v_grouped)]
            for h in range(2):
                for u in due:
                    project(u, halves=(h,))
            for u in due:
                to_project.remove(u)
            if PARKED[-1] in due:
                load_rest()
            if not other_first:
                tensor_other(s)

        first = UNITS - KG

        def quantize_and_project(u):
            new_codes(u)
            quantize_a(u)
            project(u)

        scalar_share(first)
        quantize_and_project(first - 2)
        widen_next()
        quantize_and_project(first - 1)
        to_back.extend((tiles, LAST - 2) for tiles in RESIDENT)
        back_some(len(to_back))
        widen_unit(first + 2)
        widen_next()
        weigh(LAST - 1)
        scalar_share(first + 1)
        interleave_on_gpsimd(POOL_UNITS[LAST - 1])
        widen_next()
        quantize_v(LAST - 1)
        widen_unit(UNITS - 1)
        scalar_share(first + 2)
        to_back.extend((tiles, LAST - 1) for tiles in RESIDENT)
        back_some(EARLY_SHARES)
        quantize_and_project(first)
        quantize_and_project(first + 1)

        u = UNITS - 1
        dst, src = interleave_views(u)
        nc.scalar.copy(dst[:, :, 0:2], src[:, :, 0:2])
        nc.scalar.copy(dst[:, :, 2:3], src[:, :, 2:3])
        nc.scalar.copy(w_last[:], w_sb[:, LAST:NG, 0:PACK].to_broadcast([P, P, PACK]))
        for tiles in RESIDENT + LATE:
            noise_term(tiles)
        nc.vector.tensor_copy(dst[:, :, 3:4], src[:, :, 3:4])
        new_codes(u - 1)
        quantize_a(u - 1)
        project(u - 1, halves=(0,))
        new_codes(u)
        for t0, t1 in ((3, 4), (0, 2), (2, 3)):
            quantize_a(u, t0, t1)
            project(u, range(t0, t1), closing_t=2, halves=(0,))
        project(u - 1, halves=(1,))
        project(u, halves=(1,))
        back_some(len(to_back))

        weigh(LAST)
        for h in range(2):
            quantize_v(LAST, h, h + 1)
        late = [(tiles, g) for tiles in LATE for g in range(NG)]
        for item in late[:LATE_EARLY]:
            back(*item)
        for tiles in RESIDENT:
            back(tiles, LAST)
            finish(tiles)
        for tiles, g in late[LATE_EARLY:]:
            back(tiles, g)
            if g == LAST:
                finish(tiles)
